import numpy as np, ml_dtypes
CORES = [10,34,74,98]
N = 4
BF = ml_dtypes.bfloat16
W, L, B, CAP, C, S, RO = 4096, 256, 16, 64, 8, 64, 8
def work(rng, *shape):
    return B * rng.integers(0, L, shape) + rng.integers(0, RO, shape)
def land(rng, *shape):
    return S * rng.integers(0, CAP, shape) + RO + rng.integers(0, RO, shape)
def parts(rng):
    X = rng.integers(0, 256, (N, 8, 16, W)); R = rng.integers(0, W, (N, 8, 16, W)); R = np.where(rng.random(R.shape) < 0.5, R[:, :, :1], R)
    z = rng.random((N, 8, W)); A = np.where(z < 0.3, work(rng, N, 8, W), np.where(z < 0.5, land(rng, N, 8, W), rng.integers(0, W, (N, 8, W))))
    return X, R, A, rng.integers(0, 256, (N, 8, 16)), rng.integers(1000, 1250, (N, 8, 1)) + rng.integers(0, 200, (N, 8, 16))
def pack(X, R, A, w, th):
    return {"xc": np.ascontiguousarray(X.reshape(N, 128, W)).astype(np.float32).astype(BF), "rf": np.ascontiguousarray(R.reshape(N, 128, W)).astype(np.int32),
            "an": np.ascontiguousarray(A).astype(np.int32), "w": w.reshape(N, 128, 1).astype(np.int32), "th": th.reshape(N, 128, 1).astype(np.int32)}
def setup_inputs(rng):
    return pack(*parts(rng))
def setup_inputs_copies(rng):
    X, R, A, w, th = parts(rng); x = np.arange(W)
    R[:, 1::4] = np.repeat(R[:, 1::4, :1], 16, axis=2)
    R[:, 2::4, 1:] = (R[:, 2::4, :1] + rng.integers(1, W, (N, 2, 15, W))) & (W - 1)
    A[:, ::2] = (x - B) & (W - 1)
    A[:, 1::2] = np.where(rng.random((N, 4, W)) < 0.5, land(rng, N, 4, W), work(rng, N, 4, W))
    th = rng.choice(np.array([1100, 1300, 1500]), (N, 8, 1)) + rng.integers(0, 200, (N, 8, 16))
    return pack(X, R, A, w, th)
def setup_inputs_corners(rng):
    X, R, A, w, th = parts(rng); kk = np.arange(16).reshape(1, 1, 16, 1); x = np.arange(W); heads = B * np.arange(L); off = x & (B - 1)
    X = rng.integers(0, 4, (N, 8, 16, W)); R = rng.integers(0, W, (N, 8, 16, W))
    first = R[:, :, :1]; first = np.where((first & (B - 1)) == 0, first ^ 1, first)
    R = np.where((rng.random(R.shape) < 0.5) | (kk == 0), first, R)
    R = np.where(((R + 613 * kk) & (B - 1)) == 0, R ^ 1, R)
    th = rng.integers(49, 101, (N, 8, 16)); slow = []
    for q in range(N):
        for g in range(8):
            k = int(rng.choice(np.array([0, 1, CAP - 1, CAP, CAP + 1, L])))
            if q == 0: k = (CAP, CAP + 1, L, CAP - 1, 1, 0, CAP, CAP + 1)[g]
            if q == 1: k = (CAP, CAP - 1, 1, 0, 0, 0, 0, 256 - 2 * CAP)[g]
            if q == 2: k = 31 + int(g < 7)
            if q == N - 1 and g == 7: k = CAP
            o = rng.permutation(L)
            if g == 7 and k > 0:
                i = int(np.flatnonzero(o < k)[-1]); o[[i, L - 1]] = o[[L - 1, i]]
            go = o < k; h = np.where(go, 0, rng.integers(100, 256, (16, L))); near = rng.integers(10, 13, (16, L))
            if q == 1: h = np.where(~go & (rng.random(L) < 0.5), near, h)
            if q == 2:
                h = np.where(o < 56, 0, np.where(o < 186, near, h)); slow.append(heads[(o >= k) & (o < 186)])
            X[q, g][:, heads] = h
    w[:, 0::4] = 255; w[:, 1::4] = 0; w[1:3] = 0
    A[:, 0] = x; A[:, 1] = (W - 1) * rng.integers(0, 2, (N, W)); A[:, 2] = (x + 1) & (W - 1); A[:, 3] = (x - B) & (W - 1); A[:, 5] = (x - 1) & (W - 1)
    A[:, 6] = np.where(rng.random((N, W)) < 0.5, x, W - 1 - x)
    X[2][:, :, off == 1] = rng.integers(100, 256, (8, 16, L))
    to = B * rng.integers(0, L, (8, 16, W)) + np.where(off == 2, 1, rng.integers(2, B, (8, 16, W)))
    R[2] = (to - 613 * kk[0]) & (W - 1)
    A[2] = B * rng.integers(0, L, (8, W)) + 3
    A[2][:, 2 * B * np.arange(L // 2) + 2] = 2 * B * rng.integers(0, L // 2, (8, L // 2)) + B + 2
    for g in range(8): A[2, g, slow[g]] = 2 * B * rng.integers(0, L // 2, len(slow[g])) + 2
    return pack(X, R, A, w, th)
def setup_inputs_ends(rng):
    kind = rng.integers(0, 3, (N, 8, 1, W)); X = 255 * np.where(kind == 2, rng.integers(0, 2, (N, 8, 16, W)), kind)
    R = (W - 1) * rng.integers(0, 2, (N, 8, 16, W)); A = (W - 1) * rng.integers(0, 2, (N, 8, W))
    z = rng.random((N, 8, W)); A = np.where(z < 0.12, work(rng, N, 8, W), np.where(z < 0.25, land(rng, N, 8, W), A))
    w = 255 * rng.integers(0, 2, (N, 8, 16)); th = np.zeros((N, 8, 16), np.int64)
    for q in range(N):
        many = np.append(rng.permutation(np.array([C, C - 1, C - 2, C + 1, C - 1, C, C - 1])), C)
        i = int(np.flatnonzero(many == C)[0]); many[[i, 6]] = many[[6, i]]
        for g in range(8): th[q, g, rng.permutation(16)[:many[g]]] = 4080
    w[:, 7] = 255; w[:, 6] = 0; w[:, 6, 0] = 255; w[:, 6, 1] = 1
    for x in (0, W - B):
        X[:, 7, :, x] = 255; A[:, 7, x] = 0
    X[:, 6, 0, W - B] = 16; X[:, 6, 1, W - B] = 15; A[:, 6, W - B] = W - 1; R[:, 6, 0, W - B] = 0
    X[:, 6, 0, 0] = 15; X[:, 6, 1, 0] = 250; A[:, 6, 0] = W - 2; R[:, 6, 0, 0] = 0
    R[:, 6, :, W - 1] = W - 1
    R[:, 6, :, W - 2] = W - 3
    R[:, 7, 0, 0] = W - 1; R[:, 7, 14:, 0] = 0
    X[:, 7, :, (613 * 15) & (W - 1)] = 0; X[:, 7, :, (613 * 14) & (W - 1)] = 255
    return pack(X, R, A, w, th)
def setup_inputs_spread(rng):
    X = (rng.random((N, 8, 16, W)) * np.exp2(rng.integers(0, 9, (N, 8, 1, W)))).astype(np.int64)
    p = rng.choice(np.array([1, 2, 4]), (N, 8, 16, 1)); R = np.minimum((W * rng.random((N, 8, 16, W)) ** p).astype(np.int64), W - 1)
    R = np.where(rng.random(R.shape) < rng.random((N, 8, 1, W)), R[:, :, :1], R)
    p = rng.choice(np.array([1, 2, 4]), (N, 8, 1)); A = np.minimum((W * rng.random((N, 8, W)) ** p).astype(np.int64), W - 1)
    w = np.minimum(np.exp2(8 * rng.random((N, 8, 16))).astype(np.int64), 255) * (rng.random((N, 8, 16)) > 0.1)
    p = rng.choice(np.array([1, 2, 4, 8]), (N, 8, 1)); th = np.minimum((4081 * rng.random((N, 8, 16)) ** p).astype(np.int64), 4080)
    return pack(X, R, A, w, th)
def setup_inputs_ties(rng):
    X, R, A, w, th = parts(rng)
    pool = rng.integers(0, 256, (N, 8, 16, 6)); X = np.take_along_axis(pool, rng.integers(0, 6, (N, 8, 1, W)), 3)
    i = rng.integers(0, 6, (N, 8, 1, 16)); j = rng.integers(0, 6, (N, 8, 1, 16))
    d = np.add.reduce(np.abs(np.take_along_axis(pool, i, 3) - np.take_along_axis(pool, j, 3)), axis=2)
    return pack(X, R, A, w, np.minimum(d + rng.integers(0, 2, d.shape), 4080))
def check_inputs(d):
    bad = []
    for k, lo, hi in (("xc", 0, 255), ("rf", 0, W - 1), ("an", 0, W - 1), ("w", 0, 255), ("th", 0, 4080)):
        a = np.asarray(d[k]).astype(np.float64)
        if not (np.min(a) >= lo and np.max(a) <= hi): bad.append("range of " + k)
        elif np.any(a != np.floor(a)): bad.append("whole numbers in " + k)
    return bad
def cols(T, ix):
    return np.take_along_axis(T, ix[:, :, None, :], 3)
def dist(X, q, u, m):
    kk = np.arange(16).reshape(1, 1, 16, 1); s = ((m * u >> 5) + m + 613 * kk) & (W - 1)
    x = cols(X, s.reshape(N, 8, 16 * L)).reshape(N, 8, 16, 16, L)
    return np.add.reduce(np.abs(x - q[:, :, :, None, :]), axis=2).astype(np.int64)
def reference(xc, rf, an, w, th):
    X = xc.astype(np.float32).astype(np.int32).reshape(N, 8, 16, W); R = rf.astype(np.int64).reshape(N, 8, 16, W); A = an.astype(np.int64)
    ww = w.astype(np.int64).reshape(N, 8, 16, 1); tt = th.astype(np.int64).reshape(N, 8, 16, 1)
    v = np.zeros((N, 8, 1), np.int64) + B * np.arange(L); a = np.take_along_axis(A, v, 2); b = np.zeros((N, 1, 1, 1), np.int64)
    for t in range(RO):
        q = cols(X, v); u = np.add.reduce(ww * q, axis=2, keepdims=True) & 4095
        e = cols(R, a); own = np.take_along_axis(R[:, :, 0], v, 2)[:, :, None, :]
        n = np.where(e == e[:, :, :1], own, e)
        d, d2 = dist(X, q, u, e), dist(X, q, u, n)
        f = np.where(d2 < d, n, e); f[:, :, 0] = own[:, :, 0]
        fit = (np.add.reduce((np.minimum(d, d2) < tt + b).astype(np.int64), axis=2) >= C).astype(np.int64)
        b = (np.add.reduce(fit, axis=(1, 2)) & 255).reshape(N, 1, 1, 1)
        after = np.where(fit == 1, np.take_along_axis(A, v + 1, 2), np.take_along_axis(A, a, 2))
        r, g, i = np.nonzero(fit)
        R[r, g, :, v[r, g, i]] = f[r, g, :, i]; A[r, g, v[r, g, i]] = a[r, g, i]
        before = np.add.accumulate(fit, axis=2) - fit
        r, g, i = np.nonzero((fit == 1) & (before < CAP))
        R[(r + 1 + t % (N - 1)) % N, g, :, S * before[r, g, i] + RO + t] = f[r, g, :, i]
        v = v + fit; a = after
    o = R.reshape(N, 8, 16, L, B); o = o[..., :RO // 2] + 4096 * o[..., RO // 2:RO]
    h = R.reshape(N, 8, 16, CAP, S)[..., RO:2 * RO]
    return {"yr": o.reshape(N, 128, L * (RO // 2)).astype(np.float32), "yh": h.reshape(N, 128, CAP * RO).astype(np.float32),
            "yan": A.reshape(N, 8, L, B)[..., :RO].reshape(N, 8, L * RO).astype(np.float32), "yv": v.astype(np.float32), "ya": a.astype(np.float32)}

@@ -1,0 +1,417 @@
+from concourse.bass import DstId, RemoteDMATransfer
+from concourse.mybir import AluOpType as A, AxisListType, ActivationFunctionType as F
+
+NST, CH = 8, 4
+NEG = -255.0 * 65536.0
+CBW = 768
+E_ON_S = (3,)
+O_ON_V = ()
+
+SCRATCH = {}
+for _n, _s, _d in (
+        ("XW", 12288, "bfloat16"), ("RI", 4096, "int32"), ("RW", 8192, "float32"), ("AW", 8192, "bfloat16"),
+        ("IOT", 4096, "bfloat16"), ("LOW", 4096, "bfloat16"), ("SV", 4096, "bfloat16"), ("UT", 4096, "int32"),
+        ("KOT", 4096, "float32"), ("CB", NST * CBW, "float32"), ("LAND", NST * 64, "float32"), ("PRES", NST * 64, "float32"),
+        ("GE", 4096, "bfloat16"), ("GO", 4096, "bfloat16"),
+        ("AB0", 512, "bfloat16"), ("AB1", 512, "bfloat16"), ("AB2", 512, "bfloat16"), ("AB3", 512, "bfloat16"),
+        ("AR", 512, "int32"), ("ARS", 1024, "int32"), ("ARB", 1040, "bfloat16"),
+        ("WI", 1, "int32"), ("TI", 1, "int32"), ("PI", 1, "int32"), ("PGI", 1, "int32"), ("PKI", 1, "int32"), ("KCI", 1, "int32"),
+        ("BI", 1, "int32"), ("BI2", 1, "int32"), ("COL", 32, "float32"),
+        ("CI", 144, "int32"), ("MG", 128, "int32"), ("T0", 128, "float32"), ("T1", 128, "float32"),
+        ("IDM", 128, "bfloat16"), ("NID", 128, "bfloat16"), ("Z8", 144, "bfloat16"), ("Z1", 144, "bfloat16"),
+        ("ZA", 144, "bfloat16"), ("ZB", 144, "bfloat16"), ("EQM", 128, "float32"), ("DNM", 128, "float32"),
+        ("SVE", 128, "bfloat16"), ("SVR", 128, "bfloat16"), ("SVK", 128, "bfloat16"), ("TRI", 128, "bfloat16"),
+        ("BLK", 128, "bfloat16"), ("ALL1", 128, "bfloat16"), ("WM", 128, "bfloat16"),
+        ("VI", 16, "int32"), ("KI", 16, "int32"), ("KD", 16, "float32"), ("ZERO", 16, "float32"), ("SC", 32, "float32"),
+        ("VF0", 16, "float32"), ("VF1", 16, "float32"), ("AAS", 16, "float32"), ("DA", 16, "float32"), ("MA", 16, "float32"),
+        ("AN", 16, "float32"), ("FW", 16, "bfloat16"), ("NF", 16, "float32"), ("GD", 16, "float32"), ("P1", 16, "float32"),
+        ("P2", 16, "float32"), ("DD", 16, "float32"),
+        ("A16", 16, "uint16"), ("V16", 16, "uint16"), ("D16", 16, "uint16"), ("C16", 16, "uint16"),
+        ("QG", 256, "bfloat16"), ("SVG", 256, "bfloat16"), ("AWG", 256, "bfloat16"), ("IOG", 256, "bfloat16"),
+        ("EG", 256, "float32"), ("UG", 256, "float32"), ("TA", 256, "int32"), ("TB", 256, "int32"), ("TC", 256, "int32"),
+        ("PLE", 256, "uint16"), ("PLO0", 256, "uint16"), ("PLO1", 256, "uint16"), ("UC", 256, "int32"),
+        ("OA", 256, "int32"), ("OB", 256, "int32"), ("OC", 256, "int32"),
+        ("NEQ", 256, "float32"), ("DM", 256, "float32"), ("MN", 256, "int32"), ("IND", 256, "bfloat16"), ("FV", 256, "int32"),
+        ("YH", 512, "float32"), ("YVA", 512, "float32")):
+    SCRATCH[_n] = ("sbuf", [128, _s], _d)
+for _n in ("W0", "W1", "W2", "W3", "KE", "KO", "M1", "M2"):
+    SCRATCH[_n] = ("psum", [128, 512], "float32")
+SEMAPHORES = ["qv", "qs", "qp", "qg", "pre", "sent"] + ["arr%d" % t for t in range(NST)] + ["d%d" % i for i in range(28)]
+
+
+def rank_program(g, core, T, topo):
+    rank = T.rank_of(core)
+    if rank is None:
+        return
+    n_ranks = len(T.cores)
+    queue = {"v": g.vector, "s": g.scalar, "p": g.tensor, "g": g, "y": g.sync}
+    seen = {q: {} for q in queue}
+    count = {}
+    last, readers = {}, {}
+
+    def need(q, tok):
+        s, n, clock = tok
+        if seen[q].get(s, 0) < n:
+            queue[q].wait_ge(T.sem[s], n)
+            for k, x in clock.items():
+                seen[q][k] = max(seen[q].get(k, 0), x)
+            seen[q][s] = n
+
+    def before(q, own, rd, wr):
+        for k in rd:
+            if k in last:
+                need(q, last[k])
+            if k[0] == "#":
+                for s, tok in readers.get(k, {}).items():
+                    if s != own:
+                        need(q, tok)
+        for k in wr:
+            if k in last and (q != "p" or last[k][0] != own):
+                need(q, last[k])
+            for s, tok in readers.get(k, {}).items():
+                need(q, tok)
+
+    def after(tok, rd, wr):
+        for k in wr:
+            last[k] = tok
+            readers[k] = {}
+        for k in rd:
+            readers.setdefault(k, {})[tok[0]] = tok
+
+    def split(keys):
+        return keys.split() if keys else []
+
+    def op(q, name, args, rd="", wr="", **kw):
+        rd, wr, own = split(rd), split(wr), "q" + q
+        before(q, own, rd, wr)
+        eng = queue[q]
+        fns = {"copy": ("v", lambda: eng.tensor_copy(*args)), "tt": ("v", lambda: eng.tensor_tensor(*args)),
+               "ts": ("v", lambda: eng.tensor_scalar(*args)), "act": ("s", lambda: eng.activation(*args, **kw)),
+               "mm": ("p", lambda: eng.matmul(*args)), "scan": ("v", lambda: eng.tensor_tensor_scan(*args)),
+               "red": ("v", lambda: eng.tensor_reduce(*args)), "set": ("v", lambda: eng.memset(*args)),
+               "iota": ("g", lambda: eng.iota(*args, **kw))}
+        fns[name][1]().then_inc(T.sem[own], 1)
+        count[own] = count.get(own, 0) + 1
+        after((own, count[own], dict(seen[q])), rd, wr)
+
+    dmas = [0]
+
+    def dma(q, out, in_, rd="", wr=""):
+        rd, wr = split(rd), split(wr)
+        s = "d%d" % dmas[0]
+        dmas[0] += 1
+        before(q, s, rd, wr)
+        queue[q].dma_start(out, in_).then_inc(T.sem[s], 16)
+        count[s] = 16
+        after((s, 16, dict(seen[q])), rd, wr)
+
+    def mm(out, lhs, rhs, start, stop, rd, wr):
+        op("p", "mm", (out, lhs, rhs, start, stop), rd, wr)
+
+    dma("y", T.AR[:, 0:256], T.rf[0::16, :], wr="AR0")
+    dma("y", T.AR[:, 256:512], T.an[:, :], wr="AR1")
+    dma("y", T.WI[:], T.w[:], wr="WI")
+    dma("y", T.TI[:], T.th[:], wr="TI")
+    dma("y", T.XW[:, 0:4096], T.xc[:], wr="X1")
+    dma("y", T.XW[:, 4096:8192], T.xc[:], wr="X2")
+    dma("y", T.XW[:, 8192:12288], T.xc[:], wr="X3")
+    dma("y", T.RI[:], T.rf[:], wr="RI")
+
+    op("g", "iota", (T.PI[:], [[0, 1]], 0, 1), wr="PI")
+    op("g", "iota", (T.CI[:], [[1, 144]], 0, 0), wr="CI")
+    op("g", "iota", (T.VI[:], [[256, 16]], 0, 16), wr="VI")
+    op("g", "iota", (T.KI[:], [[16, 16]], 256, 1), wr="KI")
+    op("g", "iota", (T.LOW[:], [[0, 64], [1, 64]], 0, 0), wr="LOW", allow_small_or_imprecise_dtypes=True)
+    op("g", "iota", (T.IOT[:], [[1, 64], [0, 64]], 0, 0), wr="IOT", allow_small_or_imprecise_dtypes=True)
+    dma("y", T.IOT[1::16, :], T.LOW[0:8, :], rd="LOW", wr="IOT")
+
+    ncol = {}
+
+    def col(name):
+        if name not in ncol:
+            ncol[name] = len(ncol)
+        return T.COL[:, ncol[name]:ncol[name] + 1]
+
+    def ts(out, in0, s1, s2, o0, o1, rd, wr):
+        op("v", "ts", (out, in0, s1, s2, o0) if o1 is None else (out, in0, s1, s2, o0, o1), rd, wr)
+
+    def tt(out, a, b, o, rd, wr):
+        op("v", "tt", (out, a, b, o), rd, wr)
+
+    def cp(out, in_, rd, wr):
+        op("v", "copy", (out, in_), rd, wr)
+
+    op("v", "set", (T.SV[:], 1.0), wr="SV0 SV1 SV2 SV3 SVx")
+    op("v", "set", (T.AW[:, 0:4096], 0.0), wr="AW")
+    op("v", "set", (T.ALL1[:], 1.0), wr="ALL1")
+    op("v", "set", (T.ZERO[:], 0.0), wr="ZERO")
+    op("v", "set", (T.SC[:], 0.0), wr="SC")
+    op("v", "set", (T.ARB[:, 1024:1040], 0.0), wr="pad")
+    ts(T.ARS[:, 0:512], T.AR[:], 6, None, A.arith_shift_right, None, "AR0 AR1", "ARS0")
+    ts(T.ARS[:, 512:1024], T.AR[:], 63, None, A.bitwise_and, None, "AR0 AR1", "ARS1")
+    cp(T.ARB[:, 0:1024], T.ARS[:], "ARS0 ARS1", "ARB")
+    dma("y", T.SV[0::16, :], T.ARB[:, 0:256], rd="ARB", wr="SV0")
+    dma("y", T.SV[1::16, :], T.ARB[:, 512:768], rd="ARB", wr="SV1")
+    dma("y", T.SV[2::16, :], T.ARB[:, 257:513], rd="ARB", wr="SV2")
+    dma("y", T.SV[3::16, :], T.ARB[:, 769:1025], rd="ARB pad", wr="SV3")
+    dma("y", T.AW[0::16, 0:4096], T.ARB[:, 256:512], rd="ARB", wr="AW")
+    dma("y", T.AW[1::16, 0:4096], T.ARB[:, 768:1024], rd="ARB", wr="AWr")
+    op("v", "copy", (col("p"), T.PI[:]), "PI", "c_p")
+    ts(T.PGI[:], T.PI[:], 112, None, A.bitwise_and, None, "PI", "PGI")
+    ts(T.PKI[:], T.PI[:], 15, None, A.bitwise_and, None, "PI", "PKI")
+    ts(T.MG[:], T.CI[:, 0:128], 112, None, A.bitwise_and, None, "CI", "MG")
+    cp(col("pg"), T.PGI[:], "PGI", "c_pg")
+    ts(col("pg16"), T.PGI[:], 16.0, None, A.add, None, "PGI", "c_pg16")
+    ts(col("pgx"), T.PGI[:], 16.0, None, A.mult, None, "PGI", "c_pgx")
+    ts(col("k0"), T.PKI[:], 0.0, 64.0, A.is_equal, A.mult, "PKI", "c_k0")
+    ts(col("k1"), T.PKI[:], 1.0, None, A.is_equal, None, "PKI", "c_k1")
+    ts(col("k2"), T.PKI[:], 2.0, 64.0, A.is_equal, A.mult, "PKI", "c_k2")
+    ts(col("k3"), T.PKI[:], 3.0, None, A.is_equal, None, "PKI", "c_k3")
+    ts(col("k4"), T.PKI[:], 4.0, NEG, A.is_equal, A.mult, "PKI", "c_k4")
+    ts(col("k5"), T.PKI[:], 5.0, 4096.0, A.is_equal, A.mult, "PKI", "c_k5")
+    ts(col("nk"), T.PKI[:], 0.0, None, A.is_gt, None, "PKI", "c_nk")
+    ts(T.KCI[:], T.PKI[:], 613.0, None, A.mult, None, "PKI", "KCI")
+    tt(col("kr"), col("k0"), col("k1"), A.add, "c_k0 c_k1", "c_kr")
+    tt(col("kb"), col("k2"), col("k3"), A.add, "c_k2 c_k3", "c_kb")
+    ts(T.BI[:], T.KCI[:], 4095, None, A.bitwise_and, None, "KCI", "BI")
+    tt(col("k45"), col("k4"), col("k5"), A.add, "c_k4 c_k5", "c_k45")
+    cp(col("kc"), T.BI[:], "BI", "c_kc")
+    tt(col("kk"), col("kr"), col("k45"), A.add, "c_kr c_k45", "c_kk")
+    ts(T.IDM[:], T.CI[:, 0:128], col("p"), None, A.is_equal, None, "CI c_p", "IDM")
+    ts(T.NID[:], T.CI[:, 0:128], col("p"), -1.0, A.is_equal, A.mult, "CI c_p", "NID")
+    ts(T.BLK[:], T.MG[:], col("pg"), None, A.is_equal, None, "MG c_pg", "BLK")
+    ts(T.SVR[:], T.MG[:], col("pg"), col("kr"), A.is_equal, A.mult, "MG c_pg c_kr", "SVR")
+    cp(col("w"), T.WI[:], "WI", "c_w")
+    ts(col("th"), T.TI[:], 8192.0, NEG, A.mult, A.add, "TI", "c_th")
+    ts(T.WM[:], T.MG[:], col("pg"), col("w"), A.is_equal, A.mult, "MG c_pg c_w", "WM")
+    ts(T.SVK[:], T.MG[:], col("pg"), col("kk"), A.is_equal, A.mult, "MG c_pg c_kk", "SVK")
+    ts(T.Z8[:], T.CI[:], col("pg16"), 8192.0, A.is_equal, A.mult, "CI c_pg16", "Z8")
+
+    SVall = "SV0 SV1 SV2 SV3 SVx"
+    Xall = "X1 X2 X3"
+
+    def prep_u(c):
+        mm(T.M1[:, 0:256], T.WM[:], T.XW[:, c:4096:16], True, True, "WM X1", "#M1")
+        mm(T.M1[:, 256:512], T.SVR[:], T.SV[:, c::16], True, True, "SVR " + SVall, "#M1")
+
+    def prep_v(c):
+        cp(T.UC[:], T.M1[:, 0:256], "#M1", "UC")
+        ts(T.UT[:, c::16], T.UC[:], 4095, None, A.bitwise_and, None, "UC", "UT")
+        tt(T.OA[:], T.M1[:, 256:512], T.UT[:, c::16], A.mult, "#M1 UT", "OA")
+        ts(T.OB[:], T.OA[:], 5, 4095, A.arith_shift_right, A.bitwise_and, "OA", "OB")
+        tt(T.OC[:], T.M1[:, 256:512], T.OB[:], A.add, "#M1 OB", "OC")
+        ts(T["PLO%d" % (c % 2)][:], T.OC[:], col("kc"), None, A.add, None, "OC c_kc", "PLO%d" % (c % 2))
+
+    half = [0]
+
+    def gather(e, c, q, b=0):
+        G, pl = (T.GE, "PLE") if e else (T.GO, "PLO%d" % (b % 2))
+        src = T.XW[:].indirect(T[pl][:, 64 * c:64 * c + 64])
+        out = G[:, 1024 * c:1024 * c + 1024]
+        key = ("GE%d" if e else "GO%d") % c
+        if q == "v":
+            cp(out, src, Xall + " " + pl, key)
+        else:
+            op("s", "act", (out, src, F.Copy), Xall + " " + pl, key)
+
+    pending = []
+
+    def sums(item):
+        e, c, h, w, b = item
+        K, key = (T.KE, "#KE") if e else (T.KO, "#KO")
+        o = K[:, 64 * c:64 * c + 64]
+        if h == 0:
+            if e:
+                mm(o, T.SVE[:], T.SVG[:, 64 * c:64 * c + 64], True, False, "SVE SVG", key)
+                mm(o, T.DNM[:], T.EG[:, 64 * c:64 * c + 64], False, False, "DNM EG", key)
+            else:
+                mm(o, T.SVK[:], T.SV[:, 1024 * c + b:1024 * c + 1024:16], True, False, "SVK " + SVall, key)
+        for kk in range(8):
+            k = 8 * h + kk
+            mm(o, T.Z8[:, 16 - k:144 - k], T["AB%d" % w][:, 64 * kk:64 * kk + 64], False, k == 15, "Z8 AB%d" % w, key)
+
+    def diff(e, c, h, b=0):
+        w = half[0] % 4
+        half[0] += 1
+        G, key = (T.GE, "GE%d" % c) if e else (T.GO, "GO%d" % c)
+        q, qk = (T.QG[:, 64 * c:64 * c + 64], "QG") if e else (T.XW[:, 1024 * c + b:1024 * c + 1024:16], "X1")
+        W = T["W%d" % w]
+        for kk in range(8):
+            k, o = 8 * h + kk, W[:, 64 * kk:64 * kk + 64]
+            mm(o, T.IDM[:], G[:, 1024 * c + k:1024 * c + 1024:16], True, False, "IDM " + key, "#W%d" % w)
+            mm(o, T.NID[:], q, False, True, "NID " + qk, "#W%d" % w)
+        op("s", "act", (T["AB%d" % w][:], W[:], F.Abs), "#W%d" % w, "AB%d" % w)
+        pending.append((e, c, h, w, b))
+        while len(pending) > 2:
+            sums(pending.pop(0))
+
+    def flush():
+        while pending:
+            sums(pending.pop(0))
+
+    def own_table(b):
+        op("s", "act", (T.KOT[:, b::16], T.KO[:, 0:256], F.Copy), "#KO", "KOT")
+
+    def wrap(o, Z, src, zk, sk):
+        for il in range(16):
+            mm(o, Z[:, 16 - il:144 - il], src(il), il == 0, il == 15, zk + " " + sk, "#M2")
+
+    CNT, AAW, AVW, TRI_, TOT, FITS = (T.M2[:, 256 + 16 * j:272 + 16 * j] for j in range(6))
+
+    prep_u(0)
+    prep_v(0)
+    ts(T.ZA[:], T.CI[:], col("pg16"), col("kr"), A.is_equal, A.mult, "CI c_pg16 c_kr", "ZA")
+    ts(T.VF0[:], T.VI[:], col("pgx"), None, A.subtract, None, "VI c_pgx", "VF0")
+    for c in range(CH):
+        gather(False, c, "v" if c in O_ON_V else "s", 0)
+        diff(False, c, 0, 0)
+        diff(False, c, 1, 0)
+    wrap(AAW, T.ZA, lambda il: T.AW[:, 16 * il:4096:256], "ZA", "AW AWr")
+    flush()
+    own_table(0)
+    cp(T.V16[:], T.VF0[:], "VF0", "V16")
+    cp(T.UG[:], T.UT[:, 0:4096].indirect(T.V16[:]), "UT V16", "UG")
+    cp(T.RW[:, 0:4096], T.RI[:], "RI", "RW")
+    cp(T.A16[:], AAW, "#M2", "A16")
+    ts(T.T0[:], T.MG[:], col("pg"), col("k4"), A.is_equal, A.mult, "MG c_pg c_k4", "T0")
+    ts(T.T1[:], T.CI[:, 0:128], col("pg"), col("kr"), A.is_equal, A.mult, "CI c_pg c_kr", "T1")
+    tt(T.SVE[:], T.T0[:], T.T1[:], A.add, "T0 T1", "SVE")
+    ts(T.DNM[:], T.CI[:, 0:128], col("p"), col("nk"), A.is_equal, A.mult, "CI c_p c_nk", "DNM")
+    ts(T.T0[:], T.MG[:], col("p"), None, A.is_equal, None, "MG c_p", "T0")
+    tt(T.EQM[:], T.IDM[:], T.T0[:], A.subtract, "IDM T0", "EQM")
+    ts(T.ZB[:], T.CI[:], col("pg16"), col("kb"), A.is_equal, A.mult, "CI c_pg16 c_kb", "ZB")
+    ts(T.Z1[:], T.CI[:], col("pg16"), None, A.is_equal, None, "CI c_pg16", "Z1")
+    ts(T.T1[:], T.CI[:, 0:128], col("p"), None, A.is_gt, None, "CI c_p", "T1")
+    tt(T.TRI[:], T.T1[:], T.BLK[:], A.mult, "T1 BLK", "TRI")
+    ts(T.KD[:], T.KI[:], col("pg"), 1.0 / 4096, A.subtract, A.mult, "KI c_pg", "KD")
+    for t in range(NST):
+        op("s", "act", (T.PRES[:, 64 * t:64 * t + 64], T.RW[:, 8 + t:4096:64], F.Copy), "RW", "PRES%d" % t)
+    before("g", "pre", ["PRES%d" % t for t in range(NST)], [])
+    trs = []
+    for t in range(NST):
+        src = T.cores[(rank - 1 - t % (n_ranks - 1)) % n_ranks]
+        rid, pid = topo.addr(src)[:2]
+        e = topo.engines(core, src)
+        trs.append(RemoteDMATransfer(dst_ids=[DstId(rid=rid, pnc=pid)], dma_engine_mask=1 << e[t % len(e)], remote_sem=T.sem.pre,
+                                     src=T.PRES[:, 64 * t:64 * t + 64], dst=T.CB[:, CBW * t:CBW * t + 64]))
+    g.remote_dma_fused(trs, local_sem=T.sem.sent)
+    sent = NST
+    after(("pre", NST, {}), [], ["CB%d" % t for t in range(NST)])
+    count["pre"] = NST
+
+    def smalls(with_a=True):
+        op("s", "act", (T.QG[:], T.XW[:, 0:4096].indirect(T.V16[:]), F.Copy), "X1 V16", "QG")
+        op("s", "act", (T.SVG[:], T.SV[:].indirect(T.V16[:]), F.Copy), SVall + " V16", "SVG")
+        op("s", "act", (T.IOG[:], T.IOT[:].indirect(T.A16[:]), F.Copy), "IOT A16", "IOG")
+
+    prep_u(1)
+    prep_v(1)
+
+    for t in range(NST):
+        lastep = t == NST - 1
+        vf, vn = T["VF%d" % (t % 2)], T["VF%d" % ((t + 1) % 2)]
+        vfk, vnk = "VF%d" % (t % 2), "VF%d" % ((t + 1) % 2)
+        smalls()
+        op("s", "act", (T.AWG[:], T.AW[:, 0:4096].indirect(T.A16[:]), F.Copy), "AW AWr A16", "AWG")
+        if t > 0:
+            cp(T.RW[:, 7 + t:4096:64], T.LAND[:, 64 * t - 64:64 * t], "LAND%d" % (t - 1), "RW")
+            op("s", "act", (T.YH[:, t - 1::8], T.LAND[:, 64 * t - 64:64 * t], F.Copy), "LAND%d" % (t - 1), "YH")
+        tt(T.TA[:], T.RW[:, 0:4096].indirect(T.A16[:]), T.UG[:], A.mult, "RW A16 UG", "TA")
+        op("s", "act", (T.EG[:], T.RW[:, 0:4096].indirect(T.A16[:]), F.Copy), "RW A16", "EG")
+        ts(T.TB[:], T.TA[:], 5, 4095, A.arith_shift_right, A.bitwise_and, "TA", "TB")
+        tt(T.TC[:], T.RW[:, 0:4096].indirect(T.A16[:]), T.TB[:], A.add, "RW A16 TB", "TC")
+        ts(T.PLE[:], T.TC[:], col("kc"), None, A.add, None, "TC c_kc", "PLE")
+        for c in E_ON_S:
+            gather(True, c, "s")
+        for c in range(CH):
+            if c not in E_ON_S:
+                gather(True, c, "v")
+        wrap(AVW, T.ZB, lambda il: T.SVG[:, il::16], "ZB", "SVG")
+        wrap(AAW, T.ZA, lambda il: T.AWG[:, il::16], "ZA", "AWG")
+        mm(T.M2[:, 0:256], T.EQM[:], T.EG[:], True, True, "EQM EG", "#M2")
+        order = [c for c in E_ON_S] + [c for c in range(CH) if c not in E_ON_S]
+        for c in order:
+            diff(True, c, 0)
+            diff(True, c, 1)
+        flush()
+        ts(T.NEQ[:], T.M2[:, 0:256], 0.0, 33554432.0, A.not_equal, A.mult, "#M2", "NEQ")
+        cp(T.AAS[:], AAW, "#M2", "AAS")
+        tt(T.DM[:], T.KOT[:].indirect(T.V16[:]), T.NEQ[:], A.add, "KOT V16 NEQ", "DM")
+        tt(T.DA[:], AVW, T.AAS[:], A.subtract, "#M2 AAS", "DA")
+        tt(T.MN[:], T.KE[:, 0:256], T.DM[:], A.min, "#KE DM", "MN")
+        ts(T.IND[:], T.MN[:], col("th" if t == 0 else "thb"), None, A.is_lt, None, "MN " + ("c_th" if t == 0 else "c_thb"), "IND")
+        ts(T.FV[:], T.MN[:], 4095, None, A.bitwise_and, None, "MN", "FV")
+        wrap(CNT, T.Z1, lambda il: T.IND[:, il::16], "Z1", "IND")
+        ts(T.FW[:], CNT, 7.5, None, A.is_gt, None, "#M2", "FW")
+        ts(T.NF[:], CNT, 7.5, 4096.0, A.is_lt, A.mult, "#M2", "NF")
+        mm(TOT, T.BLK[:], T.FW[:], True, True, "BLK FW", "#M2")
+        mm(TRI_, T.TRI[:], T.FW[:], True, True, "TRI FW", "#M2")
+        if not lastep:
+            mm(FITS, T.ALL1[:], T.FW[:], True, True, "ALL1 FW", "#M2")
+        tt(T.GD[:], T.NF[:], T.KD[:], A.mult, "NF KD", "GD")
+        op("v", "scan", (T.SC[:, 1:17], TOT, T.ZERO[:], 0.0, A.add, A.add), "#M2 ZERO SC", "SC")
+        tt(T.P1[:], TRI_, T.GD[:], A.add, "#M2 GD", "P1")
+        tt(T.DD[:], vf[:], T.NF[:], A.add, vfk + " NF", "DD")
+        tt(T.P2[:], T.P1[:], T.SC[:, 0:16], A.add, "P1 SC", "P2")
+        tt(T.MA[:], T.FW[:], T.DA[:], A.mult, "FW DA", "MA")
+        cp(T.C16[:], T.P2[:], "P2", "C16")
+        cp(T.D16[:], T.DD[:], "DD", "D16")
+        cp(T.CB[:, CBW * t:CBW * t + CBW].indirect(T.C16[:]), T.FV[:], "C16 FV CB%d" % t, "CB%d" % t)
+        dst = T.cores[(rank + 1 + t % (n_ranks - 1)) % n_ranks]
+        rid, pid = topo.addr(dst)[:2]
+        ne = len(topo.engines(core, dst))
+        before("g", "x", ["CB%d" % t], [])
+        g.remote_dma(T.LAND[:, 64 * t:64 * t + 64], T.CB[:, CBW * t:CBW * t + 64], T.sem["arr%d" % t], T.sem.sent, pid, rid, topo.mask(core, dst))
+        sent += ne
+        after(("arr%d" % t, ne, {}), [], ["LAND%d" % t])
+        count["arr%d" % t] = ne
+        tt(T.AN[:], T.MA[:], T.AAS[:], A.add, "MA AAS", "AN")
+        tt(vn[:], vf[:], T.FW[:], A.add, vfk + " FW", vnk)
+        cp(T.AW[:].indirect(T.D16[:]), T.IOG[:], "D16 IOG", "AW AWr")
+        cp(T.A16[:], T.AN[:], "AN", "A16")
+        cp(T.V16[:], vn[:], vnk, "V16")
+        cp(T.RW[:].indirect(T.D16[:]), T.FV[:], "D16 FV", "RW")
+        if not lastep:
+            op("v", "red", (col("bs"), FITS, AxisListType.X, A.add), "#M2", "c_bs")
+            if t + 2 < NST:
+                prep_u(t + 2)
+            cp(T.UG[:], T.UT[:, 0:4096].indirect(T.V16[:]), "UT V16", "UG")
+            cp(T.BI[:], col("bs"), "c_bs", "BI")
+            ts(T.BI2[:], T.BI[:], 255, None, A.bitwise_and, None, "BI", "BI2")
+            ts(col("thb"), T.BI2[:], 8192.0, col("th"), A.mult, A.add, "BI2 c_th", "c_thb")
+            b = t + 1
+            for c in range(CH):
+                gather(False, c, "v" if c in O_ON_V else "s", b)
+                diff(False, c, 0, b)
+                diff(False, c, 1, b)
+            flush()
+            own_table(b)
+            if t + 2 < NST:
+                prep_v(t + 2)
+
+    op("s", "act", (T.IOG[:], T.IOT[:].indirect(T.A16[:]), F.Copy), "IOT A16", "IOG")
+    cp(T.SVG[:], T.IOT[:].indirect(T.V16[:]), "IOT V16", "SVG")
+    for s in range(4):
+        op("s", "act", (T.KOT[:, 1024 + 256 * s:1280 + 256 * s], T.RW[:, 4 + s:4096:16], F.Copy), "RW", "YT%d" % s, scale=4096.0)
+    for s in range(4):
+        tt(T.KOT[:, s:1024:4], T.RW[:, s:4096:16], T.KOT[:, 1024 + 256 * s:1280 + 256 * s], A.add, "RW YT%d" % s, "YR%d" % s)
+    dma("y", T.yr[:], T.KOT[:, 0:1024], rd="YR0 YR1 YR2 YR3")
+    for s in range(8):
+        w = s % 4
+        mm(T["W%d" % w][:, 0:256], T.SVR[:], T.AW[:, s:4096:16], True, True, "SVR AW AWr", "#W%d" % w)
+        if s % 2:
+            op("s", "act", (T.KOT[:, 2048 + s::8], T["W%d" % w][:, 0:256], F.Copy), "#W%d" % w, "YAN%d" % s)
+        else:
+            cp(T.KOT[:, 2048 + s::8], T["W%d" % w][:, 0:256], "#W%d" % w, "YAN%d" % s)
+    mm(T.KO[:, 0:256], T.SVR[:], T.SVG[:], True, True, "SVR SVG", "#KO")
+    mm(T.KO[:, 256:512], T.SVR[:], T.IOG[:], True, True, "SVR IOG", "#KO")
+    op("s", "act", (T.YVA[:], T.KO[:], F.Copy), "#KO", "YVA")
+    dma("y", T.yan[:], T.KOT[0::16, 2048:4096], rd=" ".join("YAN%d" % s for s in range(8)))
+    dma("y", T.yv[:], T.YVA[0::16, 0:256], rd="YVA")
+    dma("y", T.ya[:], T.YVA[0::16, 256:512], rd="YVA")
+    op("s", "act", (T.YH[:, 7::8], T.LAND[:, 448:512], F.Copy), "LAND7", "YH")
+    dma("y", T.yh[:], T.YH[:], rd="YH")
+    count["sent"] = sent
+    for s in count:
+        if seen["g"].get(s, 0) < count[s]:
+            g.wait_ge(T.sem[s], count[s])

@@ -4,7 +4,7 @@ from concourse.mybir import AluOpType as A, AxisListType, ActivationFunctionType
 NST, CH = 8, 4
 NEG = -255.0 * 65536.0
 CBW = 768
-E_ON_S = (3,)
+E_ON_S = ()
 O_ON_V = ()
 
 SCRATCH = {}
@@ -13,7 +13,7 @@ for _n, _s, _d in (
         ("IOT", 4096, "bfloat16"), ("LOW", 4096, "bfloat16"), ("SV", 4096, "bfloat16"), ("UT", 4096, "int32"),
         ("KOT", 4096, "float32"), ("CB", NST * CBW, "float32"), ("LAND", NST * 64, "float32"), ("PRES", NST * 64, "float32"),
         ("GE", 4096, "bfloat16"), ("GO", 4096, "bfloat16"),
-        ("AB0", 512, "bfloat16"), ("AB1", 512, "bfloat16"), ("AB2", 512, "bfloat16"), ("AB3", 512, "bfloat16"),
+        ("AB0", 1024, "bfloat16"), ("AB1", 1024, "bfloat16"),
         ("AR", 512, "int32"), ("ARS", 1024, "int32"), ("ARB", 1040, "bfloat16"),
         ("WI", 1, "int32"), ("TI", 1, "int32"), ("PI", 1, "int32"), ("PGI", 1, "int32"), ("PKI", 1, "int32"), ("KCI", 1, "int32"),
         ("BI", 1, "int32"), ("BI2", 1, "int32"), ("COL", 32, "float32"),
@@ -34,8 +34,8 @@ for _n, _s, _d in (
         ("NEQ", 256, "float32"), ("DM", 256, "float32"), ("MN", 256, "int32"), ("IND", 256, "bfloat16"), ("FV", 256, "int32"),
         ("YH", 512, "float32"), ("YVA", 512, "float32")):
     SCRATCH[_n] = ("sbuf", [128, _s], _d)
-for _n in ("W0", "W1", "W2", "W3", "KE", "KO", "M1", "M2"):
-    SCRATCH[_n] = ("psum", [128, 512], "float32")
+for _n, _s in (("W0", 1024), ("W1", 1024), ("KE", 512), ("KO", 512), ("M1", 512), ("M2", 512)):
+    SCRATCH[_n] = ("psum", [128, _s], "float32")
 SEMAPHORES = ["qv", "qs", "qp", "qg", "pre", "sent"] + ["arr%d" % t for t in range(NST)] + ["d%d" % i for i in range(28)]
 
 
@@ -113,9 +113,8 @@ def rank_program(g, core, T, topo):
     dma("y", T.WI[:], T.w[:], wr="WI")
     dma("y", T.TI[:], T.th[:], wr="TI")
     dma("y", T.XW[:, 0:4096], T.xc[:], wr="X1")
-    dma("y", T.XW[:, 4096:8192], T.xc[:], wr="X2")
-    dma("y", T.XW[:, 8192:12288], T.xc[:], wr="X3")
-    dma("y", T.RI[:], T.rf[:], wr="RI")
+    for h in range(2):
+        dma("y", T.RI[:, 2048 * h:2048 * h + 2048], T.rf[:, 2048 * h:2048 * h + 2048], wr="RI%d" % h)
 
     op("g", "iota", (T.PI[:], [[0, 1]], 0, 1), wr="PI")
     op("g", "iota", (T.CI[:], [[1, 144]], 0, 0), wr="CI")
@@ -123,7 +122,6 @@ def rank_program(g, core, T, topo):
     op("g", "iota", (T.KI[:], [[16, 16]], 256, 1), wr="KI")
     op("g", "iota", (T.LOW[:], [[0, 64], [1, 64]], 0, 0), wr="LOW", allow_small_or_imprecise_dtypes=True)
     op("g", "iota", (T.IOT[:], [[1, 64], [0, 64]], 0, 0), wr="IOT", allow_small_or_imprecise_dtypes=True)
-    dma("y", T.IOT[1::16, :], T.LOW[0:8, :], rd="LOW", wr="IOT")
 
     ncol = {}
 
@@ -141,11 +139,10 @@ def rank_program(g, core, T, topo):
     def cp(out, in_, rd, wr):
         op("v", "copy", (out, in_), rd, wr)
 
-    op("v", "set", (T.SV[:], 1.0), wr="SV0 SV1 SV2 SV3 SVx")
-    op("v", "set", (T.AW[:, 0:4096], 0.0), wr="AW")
-    op("v", "set", (T.ALL1[:], 1.0), wr="ALL1")
-    op("v", "set", (T.ZERO[:], 0.0), wr="ZERO")
-    op("v", "set", (T.SC[:], 0.0), wr="SC")
+    SVall = "SV0 SV1 SV2 SV3 SVx"
+    Xall = "X1 X2 X3"
+    op("v", "set", (T.SV[:], 1.0), wr=SVall)
+    op("s", "act", (T.AW[:, 0:4096], T.SV[:], F.Copy), SVall, "AW")
     op("v", "set", (T.ARB[:, 1024:1040], 0.0), wr="pad")
     ts(T.ARS[:, 0:512], T.AR[:], 6, None, A.arith_shift_right, None, "AR0 AR1", "ARS0")
     ts(T.ARS[:, 512:1024], T.AR[:], 63, None, A.bitwise_and, None, "AR0 AR1", "ARS1")
@@ -155,7 +152,8 @@ def rank_program(g, core, T, topo):
     dma("y", T.SV[2::16, :], T.ARB[:, 257:513], rd="ARB", wr="SV2")
     dma("y", T.SV[3::16, :], T.ARB[:, 769:1025], rd="ARB pad", wr="SV3")
     dma("y", T.AW[0::16, 0:4096], T.ARB[:, 256:512], rd="ARB", wr="AW")
-    dma("y", T.AW[1::16, 0:4096], T.ARB[:, 768:1024], rd="ARB", wr="AWr")
+    dma("y", T.AW[1::16, 0:4096], T.ARB[:, 768:1024], rd="ARB AW", wr="AWr")
+    dma("y", T.IOT[1::16, :], T.LOW[0:8, :], rd="LOW", wr="IOT")
     op("v", "copy", (col("p"), T.PI[:]), "PI", "c_p")
     ts(T.PGI[:], T.PI[:], 112, None, A.bitwise_and, None, "PI", "PGI")
     ts(T.PKI[:], T.PI[:], 15, None, A.bitwise_and, None, "PI", "PKI")
@@ -187,9 +185,6 @@ def rank_program(g, core, T, topo):
     ts(T.SVK[:], T.MG[:], col("pg"), col("kk"), A.is_equal, A.mult, "MG c_pg c_kk", "SVK")
     ts(T.Z8[:], T.CI[:], col("pg16"), 8192.0, A.is_equal, A.mult, "CI c_pg16", "Z8")
 
-    SVall = "SV0 SV1 SV2 SV3 SVx"
-    Xall = "X1 X2 X3"
-
     def prep_u(c):
         mm(T.M1[:, 0:256], T.WM[:], T.XW[:, c:4096:16], True, True, "WM X1", "#M1")
         mm(T.M1[:, 256:512], T.SVR[:], T.SV[:, c::16], True, True, "SVR " + SVall, "#M1")
@@ -202,7 +197,7 @@ def rank_program(g, core, T, topo):
         tt(T.OC[:], T.M1[:, 256:512], T.OB[:], A.add, "#M1 OB", "OC")
         ts(T["PLO%d" % (c % 2)][:], T.OC[:], col("kc"), None, A.add, None, "OC c_kc", "PLO%d" % (c % 2))
 
-    half = [0]
+    turn = [0]
 
     def gather(e, c, q, b=0):
         G, pl = (T.GE, "PLE") if e else (T.GO, "PLO%d" % (b % 2))
@@ -217,37 +212,48 @@ def rank_program(g, core, T, topo):
     pending = []
 
     def sums(item):
-        e, c, h, w, b = item
+        e, c, w, b = item
         K, key = (T.KE, "#KE") if e else (T.KO, "#KO")
         o = K[:, 64 * c:64 * c + 64]
-        if h == 0:
-            if e:
+        for h in range(2):
+            if h == 0 and e:
                 mm(o, T.SVE[:], T.SVG[:, 64 * c:64 * c + 64], True, False, "SVE SVG", key)
                 mm(o, T.DNM[:], T.EG[:, 64 * c:64 * c + 64], False, False, "DNM EG", key)
-            else:
+            elif h == 0:
                 mm(o, T.SVK[:], T.SV[:, 1024 * c + b:1024 * c + 1024:16], True, False, "SVK " + SVall, key)
-        for kk in range(8):
-            k = 8 * h + kk
-            mm(o, T.Z8[:, 16 - k:144 - k], T["AB%d" % w][:, 64 * kk:64 * kk + 64], False, k == 15, "Z8 AB%d" % w, key)
+            for k in range(8 * h, 8 * h + 8):
+                mm(o, T.Z8[:, 16 - k:144 - k], T["AB%d" % w][:, 64 * k:64 * k + 64], False, k == 15, "Z8 AB%d_%d" % (w, h), key)
 
-    def diff(e, c, h, b=0):
-        w = half[0] % 4
-        half[0] += 1
+    def diff(e, c, b=0, halves=False):
+        w = turn[0] % 2
+        turn[0] += 1
         G, key = (T.GE, "GE%d" % c) if e else (T.GO, "GO%d" % c)
         q, qk = (T.QG[:, 64 * c:64 * c + 64], "QG") if e else (T.XW[:, 1024 * c + b:1024 * c + 1024:16], "X1")
-        W = T["W%d" % w]
-        for kk in range(8):
-            k, o = 8 * h + kk, W[:, 64 * kk:64 * kk + 64]
-            mm(o, T.IDM[:], G[:, 1024 * c + k:1024 * c + 1024:16], True, False, "IDM " + key, "#W%d" % w)
-            mm(o, T.NID[:], q, False, True, "NID " + qk, "#W%d" % w)
-        op("s", "act", (T["AB%d" % w][:], W[:], F.Abs), "#W%d" % w, "AB%d" % w)
-        pending.append((e, c, h, w, b))
-        while len(pending) > 2:
+        W, AB = T["W%d" % w], T["AB%d" % w]
+        for k in range(16):
+            o, wk = W[:, 64 * k:64 * k + 64], "#W%d_%d" % (w, k // 8)
+            mm(o, T.IDM[:], G[:, 1024 * c + k:1024 * c + 1024:16], True, False, "IDM " + key, wk)
+            mm(o, T.NID[:], q, False, True, "NID " + qk, wk)
+            if halves and k % 8 == 7:
+                h = k // 8
+                op("s", "act", (AB[:, 512 * h:512 * h + 512], W[:, 512 * h:512 * h + 512], F.Abs), wk, "AB%d_%d" % (w, h))
+        if not halves:
+            op("s", "act", (AB[:], W[:], F.Abs), "#W%d_0 #W%d_1" % (w, w), "AB%d_0 AB%d_1" % (w, w))
+        pending.append((e, c, w, b))
+        while len(pending) > 1:
             sums(pending.pop(0))
 
     def flush():
         while pending:
             sums(pending.pop(0))
+
+    def own_unit(b):
+        for c in range(CH + 1):
+            if c < CH:
+                gather(False, c, "v" if c in O_ON_V else "s", b)
+            if c:
+                diff(False, c - 1, b)
+        flush()
 
     def own_table(b):
         op("s", "act", (T.KOT[:, b::16], T.KO[:, 0:256], F.Copy), "#KO", "KOT")
@@ -258,21 +264,47 @@ def rank_program(g, core, T, topo):
 
     CNT, AAW, AVW, TRI_, TOT, FITS = (T.M2[:, 256 + 16 * j:272 + 16 * j] for j in range(6))
 
+    def smalls():
+        op("s", "act", (T.QG[:], T.XW[:, 0:4096].indirect(T.V16[:]), F.Copy), "X1 V16", "QG")
+        op("s", "act", (T.AWG[:], T.AW[:, 0:4096].indirect(T.A16[:]), F.Copy), "AW AWr A16", "AWG")
+        op("s", "act", (T.SVG[:], T.SV[:].indirect(T.V16[:]), F.Copy), SVall + " V16", "SVG")
+
+    def place_e():
+        tt(T.TA[:], T.RW[:, 0:4096].indirect(T.A16[:]), T.UG[:], A.mult, "RW A16 UG", "TA")
+        op("s", "act", (T.EG[:], T.RW[:, 0:4096].indirect(T.A16[:]), F.Copy), "RW A16", "EG")
+        ts(T.TB[:], T.TA[:], 5, 4095, A.arith_shift_right, A.bitwise_and, "TA", "TB")
+        tt(T.TC[:], T.RW[:, 0:4096].indirect(T.A16[:]), T.TB[:], A.add, "RW A16 TB", "TC")
+        ts(T.PLE[:], T.TC[:], col("kc"), None, A.add, None, "TC c_kc", "PLE")
+
+    def gathers_e():
+        for c in E_ON_S:
+            gather(True, c, "s")
+        for c in range(CH):
+            if c not in E_ON_S:
+                gather(True, c, "v")
+
     prep_u(0)
     prep_v(0)
     ts(T.ZA[:], T.CI[:], col("pg16"), col("kr"), A.is_equal, A.mult, "CI c_pg16 c_kr", "ZA")
     ts(T.VF0[:], T.VI[:], col("pgx"), None, A.subtract, None, "VI c_pgx", "VF0")
-    for c in range(CH):
-        gather(False, c, "v" if c in O_ON_V else "s", 0)
-        diff(False, c, 0, 0)
-        diff(False, c, 1, 0)
     wrap(AAW, T.ZA, lambda il: T.AW[:, 16 * il:4096:256], "ZA", "AW AWr")
-    flush()
-    own_table(0)
+    op("s", "act", (T.XW[:, 4096:8192], T.XW[:, 0:4096], F.Copy), "X1", "X2")
+    cp(T.XW[:, 8192:12288], T.XW[:, 0:4096], "X1", "X3")
     cp(T.V16[:], T.VF0[:], "VF0", "V16")
     cp(T.UG[:], T.UT[:, 0:4096].indirect(T.V16[:]), "UT V16", "UG")
-    cp(T.RW[:, 0:4096], T.RI[:], "RI", "RW")
     cp(T.A16[:], AAW, "#M2", "A16")
+    for h in range(2):
+        cp(T.RW[:, 2048 * h:2048 * h + 2048], T.RI[:, 2048 * h:2048 * h + 2048], "RI%d" % h, "RW")
+    own_unit(0)
+    own_table(0)
+    smalls()
+    place_e()
+    gathers_e()
+    prep_u(1)
+    prep_v(1)
+    op("v", "set", (T.ALL1[:], 1.0), wr="ALL1")
+    op("v", "set", (T.ZERO[:], 0.0), wr="ZERO")
+    op("v", "set", (T.SC[:], 0.0), wr="SC")
     ts(T.T0[:], T.MG[:], col("pg"), col("k4"), A.is_equal, A.mult, "MG c_pg c_k4", "T0")
     ts(T.T1[:], T.CI[:, 0:128], col("pg"), col("kr"), A.is_equal, A.mult, "CI c_pg c_kr", "T1")
     tt(T.SVE[:], T.T0[:], T.T1[:], A.add, "T0 T1", "SVE")
@@ -299,40 +331,27 @@ def rank_program(g, core, T, topo):
     after(("pre", NST, {}), [], ["CB%d" % t for t in range(NST)])
     count["pre"] = NST
 
-    def smalls(with_a=True):
-        op("s", "act", (T.QG[:], T.XW[:, 0:4096].indirect(T.V16[:]), F.Copy), "X1 V16", "QG")
-        op("s", "act", (T.SVG[:], T.SV[:].indirect(T.V16[:]), F.Copy), SVall + " V16", "SVG")
-        op("s", "act", (T.IOG[:], T.IOT[:].indirect(T.A16[:]), F.Copy), "IOT A16", "IOG")
-
-    prep_u(1)
-    prep_v(1)
-
     for t in range(NST):
         lastep = t == NST - 1
         vf, vn = T["VF%d" % (t % 2)], T["VF%d" % ((t + 1) % 2)]
         vfk, vnk = "VF%d" % (t % 2), "VF%d" % ((t + 1) % 2)
-        smalls()
-        op("s", "act", (T.AWG[:], T.AW[:, 0:4096].indirect(T.A16[:]), F.Copy), "AW AWr A16", "AWG")
         if t > 0:
+            smalls()
             cp(T.RW[:, 7 + t:4096:64], T.LAND[:, 64 * t - 64:64 * t], "LAND%d" % (t - 1), "RW")
+            place_e()
             op("s", "act", (T.YH[:, t - 1::8], T.LAND[:, 64 * t - 64:64 * t], F.Copy), "LAND%d" % (t - 1), "YH")
-        tt(T.TA[:], T.RW[:, 0:4096].indirect(T.A16[:]), T.UG[:], A.mult, "RW A16 UG", "TA")
-        op("s", "act", (T.EG[:], T.RW[:, 0:4096].indirect(T.A16[:]), F.Copy), "RW A16", "EG")
-        ts(T.TB[:], T.TA[:], 5, 4095, A.arith_shift_right, A.bitwise_and, "TA", "TB")
-        tt(T.TC[:], T.RW[:, 0:4096].indirect(T.A16[:]), T.TB[:], A.add, "RW A16 TB", "TC")
-        ts(T.PLE[:], T.TC[:], col("kc"), None, A.add, None, "TC c_kc", "PLE")
-        for c in E_ON_S:
-            gather(True, c, "s")
-        for c in range(CH):
-            if c not in E_ON_S:
-                gather(True, c, "v")
+            gathers_e()
+            if t + 1 < NST:
+                prep_u(t + 1)
+                prep_v(t + 1)
         wrap(AVW, T.ZB, lambda il: T.SVG[:, il::16], "ZB", "SVG")
         wrap(AAW, T.ZA, lambda il: T.AWG[:, il::16], "ZA", "AWG")
         mm(T.M2[:, 0:256], T.EQM[:], T.EG[:], True, True, "EQM EG", "#M2")
         order = [c for c in E_ON_S] + [c for c in range(CH) if c not in E_ON_S]
         for c in order:
-            diff(True, c, 0)
-            diff(True, c, 1)
+            diff(True, c, 0, c == order[-1])
+            if c == order[0]:
+                op("s", "act", (T.IOG[:], T.IOT[:].indirect(T.A16[:]), F.Copy), "IOT A16", "IOG")
         flush()
         ts(T.NEQ[:], T.M2[:, 0:256], 0.0, 33554432.0, A.not_equal, A.mult, "#M2", "NEQ")
         cp(T.AAS[:], AAW, "#M2", "AAS")
@@ -373,21 +392,12 @@ def rank_program(g, core, T, topo):
         cp(T.RW[:].indirect(T.D16[:]), T.FV[:], "D16 FV", "RW")
         if not lastep:
             op("v", "red", (col("bs"), FITS, AxisListType.X, A.add), "#M2", "c_bs")
-            if t + 2 < NST:
-                prep_u(t + 2)
             cp(T.UG[:], T.UT[:, 0:4096].indirect(T.V16[:]), "UT V16", "UG")
             cp(T.BI[:], col("bs"), "c_bs", "BI")
             ts(T.BI2[:], T.BI[:], 255, None, A.bitwise_and, None, "BI", "BI2")
             ts(col("thb"), T.BI2[:], 8192.0, col("th"), A.mult, A.add, "BI2 c_th", "c_thb")
-            b = t + 1
-            for c in range(CH):
-                gather(False, c, "v" if c in O_ON_V else "s", b)
-                diff(False, c, 0, b)
-                diff(False, c, 1, b)
-            flush()
-            own_table(b)
-            if t + 2 < NST:
-                prep_v(t + 2)
+            own_unit(t + 1)
+            own_table(t + 1)
 
     op("s", "act", (T.IOG[:], T.IOT[:].indirect(T.A16[:]), F.Copy), "IOT A16", "IOG")
     cp(T.SVG[:], T.IOT[:].indirect(T.V16[:]), "IOT V16", "SVG")
@@ -397,12 +407,13 @@ def rank_program(g, core, T, topo):
         tt(T.KOT[:, s:1024:4], T.RW[:, s:4096:16], T.KOT[:, 1024 + 256 * s:1280 + 256 * s], A.add, "RW YT%d" % s, "YR%d" % s)
     dma("y", T.yr[:], T.KOT[:, 0:1024], rd="YR0 YR1 YR2 YR3")
     for s in range(8):
-        w = s % 4
-        mm(T["W%d" % w][:, 0:256], T.SVR[:], T.AW[:, s:4096:16], True, True, "SVR AW AWr", "#W%d" % w)
-        if s % 2:
-            op("s", "act", (T.KOT[:, 2048 + s::8], T["W%d" % w][:, 0:256], F.Copy), "#W%d" % w, "YAN%d" % s)
+        w, h = s // 2 % 2, s % 2
+        o, wk = T["W%d" % w][:, 512 * h:512 * h + 256], "#W%d_%d" % (w, h)
+        mm(o, T.SVR[:], T.AW[:, s:4096:16], True, True, "SVR AW AWr", wk)
+        if h:
+            op("s", "act", (T.KOT[:, 2048 + s::8], o, F.Copy), wk, "YAN%d" % s)
         else:
-            cp(T.KOT[:, 2048 + s::8], T["W%d" % w][:, 0:256], "#W%d" % w, "YAN%d" % s)
+            cp(T.KOT[:, 2048 + s::8], o, wk, "YAN%d" % s)
     mm(T.KO[:, 0:256], T.SVR[:], T.SVG[:], True, True, "SVR SVG", "#KO")
     mm(T.KO[:, 256:512], T.SVR[:], T.IOG[:], True, True, "SVR IOG", "#KO")
     op("s", "act", (T.YVA[:], T.KO[:], F.Copy), "#KO", "YVA")

@@ -2,6 +2,7 @@ from concourse.bass import DstId, RemoteDMATransfer
 from concourse.mybir import AluOpType as A, AxisListType, ActivationFunctionType as F
 
 NST, CH = 8, 4
+HOOK, WHOOK, EHOOK, EQ_AFTER = 3, 4, 4, 2
 NEG = -255.0 * 65536.0
 CBW = 768
 E_ON_S = ()
@@ -25,7 +26,7 @@ for _n, _s, _d in (
         ("VI", 16, "int32"), ("KI", 16, "int32"), ("KD", 16, "float32"), ("ZERO", 16, "float32"), ("SC", 32, "float32"),
         ("VF0", 16, "float32"), ("VF1", 16, "float32"), ("AAS", 16, "float32"), ("DA", 16, "float32"), ("MA", 16, "float32"),
         ("AN", 16, "float32"), ("FW", 16, "bfloat16"), ("NF", 16, "float32"), ("GD", 16, "float32"), ("P1", 16, "float32"),
-        ("P2", 16, "float32"), ("DD", 16, "float32"),
+        ("P2", 16, "float32"), ("DD", 16, "float32"), ("JK", 16, "float32"),
         ("A16", 16, "uint16"), ("V16", 16, "uint16"), ("D16", 16, "uint16"), ("C16", 16, "uint16"),
         ("QG", 256, "bfloat16"), ("SVG", 256, "bfloat16"), ("AWG", 256, "bfloat16"), ("IOG", 256, "bfloat16"),
         ("EG", 256, "float32"), ("UG", 256, "float32"), ("TA", 256, "int32"), ("TB", 256, "int32"), ("TC", 256, "int32"),
@@ -113,6 +114,7 @@ def rank_program(g, core, T, topo):
     dma("y", T.WI[:], T.w[:], wr="WI")
     dma("y", T.TI[:], T.th[:], wr="TI")
     dma("y", T.XW[:, 0:4096], T.xc[:], wr="X1")
+    dma("y", T.XW[:, 8192:12288], T.xc[:], wr="X3")
     for h in range(2):
         dma("y", T.RI[:, 2048 * h:2048 * h + 2048], T.rf[:, 2048 * h:2048 * h + 2048], wr="RI%d" % h)
 
@@ -142,7 +144,7 @@ def rank_program(g, core, T, topo):
     SVall = "SV0 SV1 SV2 SV3 SVx"
     Xall = "X1 X2 X3"
     op("v", "set", (T.SV[:], 1.0), wr=SVall)
-    op("s", "act", (T.AW[:, 0:4096], T.SV[:], F.Copy), SVall, "AW")
+    op("s", "act", (T.AW[:, 0:4096], T.SV[:], F.Copy), SVall, "AW AWr")
     op("v", "set", (T.ARB[:, 1024:1040], 0.0), wr="pad")
     ts(T.ARS[:, 0:512], T.AR[:], 6, None, A.arith_shift_right, None, "AR0 AR1", "ARS0")
     ts(T.ARS[:, 512:1024], T.AR[:], 63, None, A.bitwise_and, None, "AR0 AR1", "ARS1")
@@ -152,7 +154,7 @@ def rank_program(g, core, T, topo):
     dma("y", T.SV[2::16, :], T.ARB[:, 257:513], rd="ARB", wr="SV2")
     dma("y", T.SV[3::16, :], T.ARB[:, 769:1025], rd="ARB pad", wr="SV3")
     dma("y", T.AW[0::16, 0:4096], T.ARB[:, 256:512], rd="ARB", wr="AW")
-    dma("y", T.AW[1::16, 0:4096], T.ARB[:, 768:1024], rd="ARB AW", wr="AWr")
+    dma("y", T.AW[1::16, 0:4096], T.ARB[:, 768:1024], rd="ARB", wr="AWr")
     dma("y", T.IOT[1::16, :], T.LOW[0:8, :], rd="LOW", wr="IOT")
     op("v", "copy", (col("p"), T.PI[:]), "PI", "c_p")
     ts(T.PGI[:], T.PI[:], 112, None, A.bitwise_and, None, "PI", "PGI")
@@ -247,13 +249,15 @@ def rank_program(g, core, T, topo):
         while pending:
             sums(pending.pop(0))
 
-    def own_unit(b):
+    def own_unit(b, hooks):
         for c in range(CH + 1):
+            for at, f in hooks:
+                if at == c:
+                    f()
             if c < CH:
                 gather(False, c, "v" if c in O_ON_V else "s", b)
             if c:
                 diff(False, c - 1, b)
-        flush()
 
     def own_table(b):
         op("s", "act", (T.KOT[:, b::16], T.KO[:, 0:256], F.Copy), "#KO", "KOT")
@@ -269,12 +273,26 @@ def rank_program(g, core, T, topo):
         op("s", "act", (T.AWG[:], T.AW[:, 0:4096].indirect(T.A16[:]), F.Copy), "AW AWr A16", "AWG")
         op("s", "act", (T.SVG[:], T.SV[:].indirect(T.V16[:]), F.Copy), SVall + " V16", "SVG")
 
+    def wraps():
+        wrap(AVW, T.ZB, lambda il: T.SVG[:, il::16], "ZB", "SVG")
+        wrap(AAW, T.ZA, lambda il: T.AWG[:, il::16], "ZA", "AWG")
+        op("s", "act", (T.AAS[:], AAW, F.Copy), "#M2", "AAS")
+
+    def fits():
+        op("s", "act", (T.JK[:], FITS, F.Copy), "#M2", "JK c_bs", accum_out=col("bs"))
+
     def place_e():
         tt(T.TA[:], T.RW[:, 0:4096].indirect(T.A16[:]), T.UG[:], A.mult, "RW A16 UG", "TA")
         op("s", "act", (T.EG[:], T.RW[:, 0:4096].indirect(T.A16[:]), F.Copy), "RW A16", "EG")
         ts(T.TB[:], T.TA[:], 5, 4095, A.arith_shift_right, A.bitwise_and, "TA", "TB")
         tt(T.TC[:], T.RW[:, 0:4096].indirect(T.A16[:]), T.TB[:], A.add, "RW A16 TB", "TC")
         ts(T.PLE[:], T.TC[:], col("kc"), None, A.add, None, "TC c_kc", "PLE")
+
+    def merge(t):
+        cp(T.RW[:, 8 + t:4096:64], T.LAND[:, 64 * t:64 * t + 64], "LAND%d" % t, "RW")
+
+    def keep_yh(t):
+        op("s", "act", (T.YH[:, t::8], T.LAND[:, 64 * t:64 * t + 64], F.Copy), "LAND%d" % t, "YH")
 
     def gathers_e():
         for c in E_ON_S:
@@ -289,22 +307,12 @@ def rank_program(g, core, T, topo):
     ts(T.VF0[:], T.VI[:], col("pgx"), None, A.subtract, None, "VI c_pgx", "VF0")
     wrap(AAW, T.ZA, lambda il: T.AW[:, 16 * il:4096:256], "ZA", "AW AWr")
     op("s", "act", (T.XW[:, 4096:8192], T.XW[:, 0:4096], F.Copy), "X1", "X2")
-    cp(T.XW[:, 8192:12288], T.XW[:, 0:4096], "X1", "X3")
     cp(T.V16[:], T.VF0[:], "VF0", "V16")
     cp(T.UG[:], T.UT[:, 0:4096].indirect(T.V16[:]), "UT V16", "UG")
     cp(T.A16[:], AAW, "#M2", "A16")
     for h in range(2):
         cp(T.RW[:, 2048 * h:2048 * h + 2048], T.RI[:, 2048 * h:2048 * h + 2048], "RI%d" % h, "RW")
-    own_unit(0)
-    own_table(0)
-    smalls()
-    place_e()
-    gathers_e()
-    prep_u(1)
-    prep_v(1)
-    op("v", "set", (T.ALL1[:], 1.0), wr="ALL1")
-    op("v", "set", (T.ZERO[:], 0.0), wr="ZERO")
-    op("v", "set", (T.SC[:], 0.0), wr="SC")
+    own_unit(0, [(3, smalls), (4, place_e), (4, gathers_e)])
     ts(T.T0[:], T.MG[:], col("pg"), col("k4"), A.is_equal, A.mult, "MG c_pg c_k4", "T0")
     ts(T.T1[:], T.CI[:, 0:128], col("pg"), col("kr"), A.is_equal, A.mult, "CI c_pg c_kr", "T1")
     tt(T.SVE[:], T.T0[:], T.T1[:], A.add, "T0 T1", "SVE")
@@ -312,6 +320,11 @@ def rank_program(g, core, T, topo):
     ts(T.T0[:], T.MG[:], col("p"), None, A.is_equal, None, "MG c_p", "T0")
     tt(T.EQM[:], T.IDM[:], T.T0[:], A.subtract, "IDM T0", "EQM")
     ts(T.ZB[:], T.CI[:], col("pg16"), col("kb"), A.is_equal, A.mult, "CI c_pg16 c_kb", "ZB")
+    prep_u(1)
+    prep_v(1)
+    op("v", "set", (T.ALL1[:], 1.0), wr="ALL1")
+    op("v", "set", (T.ZERO[:], 0.0), wr="ZERO")
+    op("v", "set", (T.SC[:], 0.0), wr="SC")
     ts(T.Z1[:], T.CI[:], col("pg16"), None, A.is_equal, None, "CI c_pg16", "Z1")
     ts(T.T1[:], T.CI[:, 0:128], col("p"), None, A.is_gt, None, "CI c_p", "T1")
     tt(T.TRI[:], T.T1[:], T.BLK[:], A.mult, "T1 BLK", "TRI")
@@ -335,26 +348,25 @@ def rank_program(g, core, T, topo):
         lastep = t == NST - 1
         vf, vn = T["VF%d" % (t % 2)], T["VF%d" % ((t + 1) % 2)]
         vfk, vnk = "VF%d" % (t % 2), "VF%d" % ((t + 1) % 2)
+        if t > 0 and t + 1 < NST:
+            prep_u(t + 1)
+            prep_v(t + 1)
         if t > 0:
-            smalls()
-            cp(T.RW[:, 7 + t:4096:64], T.LAND[:, 64 * t - 64:64 * t], "LAND%d" % (t - 1), "RW")
-            place_e()
-            op("s", "act", (T.YH[:, t - 1::8], T.LAND[:, 64 * t - 64:64 * t], F.Copy), "LAND%d" % (t - 1), "YH")
-            gathers_e()
-            if t + 1 < NST:
-                prep_u(t + 1)
-                prep_v(t + 1)
-        wrap(AVW, T.ZB, lambda il: T.SVG[:, il::16], "ZB", "SVG")
-        wrap(AAW, T.ZA, lambda il: T.AWG[:, il::16], "ZA", "AWG")
-        mm(T.M2[:, 0:256], T.EQM[:], T.EG[:], True, True, "EQM EG", "#M2")
+            cp(T.BI[:], col("bs"), "c_bs", "BI")
+            ts(T.BI2[:], T.BI[:], 255, None, A.bitwise_and, None, "BI", "BI2")
+            ts(col("thb"), T.BI2[:], 8192.0, col("th"), A.mult, A.add, "BI2 c_th", "c_thb")
         order = [c for c in E_ON_S] + [c for c in range(CH) if c not in E_ON_S]
         for c in order:
             diff(True, c, 0, c == order[-1])
             if c == order[0]:
+                own_table(t)
                 op("s", "act", (T.IOG[:], T.IOT[:].indirect(T.A16[:]), F.Copy), "IOT A16", "IOG")
+            if c == order[EQ_AFTER]:
+                if t == 0:
+                    wraps()
+                mm(T.M2[:, 0:256], T.EQM[:], T.EG[:], True, True, "EQM EG", "#M2")
+                op("s", "act", (T.NEQ[:], T.M2[:, 0:256], F.Abs), "#M2", "NEQ", scale=33554432.0)
         flush()
-        ts(T.NEQ[:], T.M2[:, 0:256], 0.0, 33554432.0, A.not_equal, A.mult, "#M2", "NEQ")
-        cp(T.AAS[:], AAW, "#M2", "AAS")
         tt(T.DM[:], T.KOT[:].indirect(T.V16[:]), T.NEQ[:], A.add, "KOT V16 NEQ", "DM")
         tt(T.DA[:], AVW, T.AAS[:], A.subtract, "#M2 AAS", "DA")
         tt(T.MN[:], T.KE[:, 0:256], T.DM[:], A.min, "#KE DM", "MN")
@@ -384,28 +396,28 @@ def rank_program(g, core, T, topo):
         sent += ne
         after(("arr%d" % t, ne, {}), [], ["LAND%d" % t])
         count["arr%d" % t] = ne
+        if lastep:
+            cp(T.RW[:].indirect(T.D16[:]), T.FV[:], "D16 FV", "RW")
         tt(T.AN[:], T.MA[:], T.AAS[:], A.add, "MA AAS", "AN")
         tt(vn[:], vf[:], T.FW[:], A.add, vfk + " FW", vnk)
         cp(T.AW[:].indirect(T.D16[:]), T.IOG[:], "D16 IOG", "AW AWr")
         cp(T.A16[:], T.AN[:], "AN", "A16")
         cp(T.V16[:], vn[:], vnk, "V16")
-        cp(T.RW[:].indirect(T.D16[:]), T.FV[:], "D16 FV", "RW")
         if not lastep:
-            op("v", "red", (col("bs"), FITS, AxisListType.X, A.add), "#M2", "c_bs")
+            cp(T.RW[:].indirect(T.D16[:]), T.FV[:], "D16 FV", "RW")
             cp(T.UG[:], T.UT[:, 0:4096].indirect(T.V16[:]), "UT V16", "UG")
-            cp(T.BI[:], col("bs"), "c_bs", "BI")
-            ts(T.BI2[:], T.BI[:], 255, None, A.bitwise_and, None, "BI", "BI2")
-            ts(col("thb"), T.BI2[:], 8192.0, col("th"), A.mult, A.add, "BI2 c_th", "c_thb")
-            own_unit(t + 1)
-            own_table(t + 1)
+            own_unit(t + 1, [(2, fits), (HOOK, smalls), (WHOOK, wraps), (EHOOK, lambda: merge(t)), (EHOOK, place_e), (EHOOK, gathers_e), (4, lambda: keep_yh(t))])
 
+    for s in range(4):
+        w, h = s // 2, s % 2
+        o, wk = T["W%d" % w][:, 512 * h:512 * h + 256], "#W%d_%d" % (w, h)
+        op("s", "act", (o, T.RW[:, 4 + s:4096:16], F.Copy), "RW", wk, scale=4096.0)
+        tt(T.KOT[:, s:1024:4], o, T.RW[:, s:4096:16], A.add, "RW " + wk, "YR%d" % s)
+    dma("y", T.yr[:], T.KOT[:, 0:1024], rd="YR0 YR1 YR2 YR3")
     op("s", "act", (T.IOG[:], T.IOT[:].indirect(T.A16[:]), F.Copy), "IOT A16", "IOG")
     cp(T.SVG[:], T.IOT[:].indirect(T.V16[:]), "IOT V16", "SVG")
-    for s in range(4):
-        op("s", "act", (T.KOT[:, 1024 + 256 * s:1280 + 256 * s], T.RW[:, 4 + s:4096:16], F.Copy), "RW", "YT%d" % s, scale=4096.0)
-    for s in range(4):
-        tt(T.KOT[:, s:1024:4], T.RW[:, s:4096:16], T.KOT[:, 1024 + 256 * s:1280 + 256 * s], A.add, "RW YT%d" % s, "YR%d" % s)
-    dma("y", T.yr[:], T.KOT[:, 0:1024], rd="YR0 YR1 YR2 YR3")
+    keep_yh(NST - 1)
+    dma("y", T.yh[:], T.YH[:], rd="YH")
     for s in range(8):
         w, h = s // 2 % 2, s % 2
         o, wk = T["W%d" % w][:, 512 * h:512 * h + 256], "#W%d_%d" % (w, h)
@@ -420,8 +432,6 @@ def rank_program(g, core, T, topo):
     dma("y", T.yan[:], T.KOT[0::16, 2048:4096], rd=" ".join("YAN%d" % s for s in range(8)))
     dma("y", T.yv[:], T.YVA[0::16, 0:256], rd="YVA")
     dma("y", T.ya[:], T.YVA[0::16, 256:512], rd="YVA")
-    op("s", "act", (T.YH[:, 7::8], T.LAND[:, 448:512], F.Copy), "LAND7", "YH")
-    dma("y", T.yh[:], T.YH[:], rd="YH")
     count["sent"] = sent
     for s in count:
         if seen["g"].get(s, 0) < count[s]:

from concourse.bass import DstId, RemoteDMATransfer
from concourse.mybir import AluOpType as A, AxisListType, ActivationFunctionType as F

NST, CH = 8, 4
HOOK, WHOOK, EHOOK, EQ_AFTER = 3, 4, 4, 2
NEG = -255.0 * 65536.0
CBW = 768
E_ON_S = ()
O_ON_V = ()

SCRATCH = {}
for _n, _s, _d in (
        ("XW", 12288, "bfloat16"), ("RI", 4096, "int32"), ("RW", 8192, "float32"), ("AW", 8192, "bfloat16"),
        ("IOT", 4096, "bfloat16"), ("LOW", 4096, "bfloat16"), ("SV", 4096, "bfloat16"), ("UT", 4096, "int32"),
        ("KOT", 4096, "float32"), ("CB", NST * CBW, "float32"), ("LAND", NST * 64, "float32"), ("PRES", NST * 64, "float32"),
        ("GE", 4096, "bfloat16"), ("GO", 4096, "bfloat16"),
        ("AB0", 1024, "bfloat16"), ("AB1", 1024, "bfloat16"),
        ("AR", 512, "int32"), ("ARS", 1024, "int32"), ("ARB", 1040, "bfloat16"),
        ("WI", 1, "int32"), ("TI", 1, "int32"), ("PI", 1, "int32"), ("PGI", 1, "int32"), ("PKI", 1, "int32"), ("KCI", 1, "int32"),
        ("BI", 1, "int32"), ("BI2", 1, "int32"), ("COL", 32, "float32"),
        ("CI", 144, "int32"), ("MG", 128, "int32"), ("T0", 128, "float32"), ("T1", 128, "float32"),
        ("IDM", 128, "bfloat16"), ("NID", 128, "bfloat16"), ("Z8", 144, "bfloat16"), ("Z1", 144, "bfloat16"),
        ("ZA", 144, "bfloat16"), ("ZB", 144, "bfloat16"), ("EQM", 128, "float32"), ("DNM", 128, "float32"),
        ("SVE", 128, "bfloat16"), ("SVR", 128, "bfloat16"), ("SVK", 128, "bfloat16"), ("TRI", 128, "bfloat16"),
        ("BLK", 128, "bfloat16"), ("ALL1", 128, "bfloat16"), ("WM", 128, "bfloat16"),
        ("VI", 16, "int32"), ("KI", 16, "int32"), ("KD", 16, "float32"), ("ZERO", 16, "float32"), ("SC", 32, "float32"),
        ("VF0", 16, "float32"), ("VF1", 16, "float32"), ("AAS", 16, "float32"), ("DA", 16, "float32"), ("MA", 16, "float32"),
        ("AN", 16, "float32"), ("FW", 16, "bfloat16"), ("NF", 16, "float32"), ("GD", 16, "float32"), ("P1", 16, "float32"),
        ("P2", 16, "float32"), ("DD", 16, "float32"), ("JK", 16, "float32"),
        ("A16", 16, "uint16"), ("V16", 16, "uint16"), ("D16", 16, "uint16"), ("C16", 16, "uint16"),
        ("QG", 256, "bfloat16"), ("SVG", 256, "bfloat16"), ("AWG", 256, "bfloat16"), ("IOG", 256, "bfloat16"),
        ("EG", 256, "float32"), ("UG", 256, "float32"), ("TA", 256, "int32"), ("TB", 256, "int32"), ("TC", 256, "int32"),
        ("PLE", 256, "uint16"), ("PLO0", 256, "uint16"), ("PLO1", 256, "uint16"), ("UC", 256, "int32"),
        ("OA", 256, "int32"), ("OB", 256, "int32"), ("OC", 256, "int32"),
        ("NEQ", 256, "float32"), ("DM", 256, "float32"), ("MN", 256, "int32"), ("IND", 256, "bfloat16"), ("FV", 256, "int32"),
        ("YH", 512, "float32"), ("YVA", 512, "float32")):
    SCRATCH[_n] = ("sbuf", [128, _s], _d)
for _n, _s in (("W0", 1024), ("W1", 1024), ("KE", 512), ("KO", 512), ("M1", 512), ("M2", 512)):
    SCRATCH[_n] = ("psum", [128, _s], "float32")
SEMAPHORES = ["qv", "qs", "qp", "qg", "pre", "sent"] + ["arr%d" % t for t in range(NST)] + ["d%d" % i for i in range(28)]


def rank_program(g, core, T, topo):
    rank = T.rank_of(core)
    if rank is None:
        return
    n_ranks = len(T.cores)
    queue = {"v": g.vector, "s": g.scalar, "p": g.tensor, "g": g, "y": g.sync}
    seen = {q: {} for q in queue}
    count = {}
    last, readers = {}, {}

    def need(q, tok):
        s, n, clock = tok
        if seen[q].get(s, 0) < n:
            queue[q].wait_ge(T.sem[s], n)
            for k, x in clock.items():
                seen[q][k] = max(seen[q].get(k, 0), x)
            seen[q][s] = n

    def before(q, own, rd, wr):
        for k in rd:
            if k in last:
                need(q, last[k])
            if k[0] == "#":
                for s, tok in readers.get(k, {}).items():
                    if s != own:
                        need(q, tok)
        for k in wr:
            if k in last and (q != "p" or last[k][0] != own):
                need(q, last[k])
            for s, tok in readers.get(k, {}).items():
                need(q, tok)

    def after(tok, rd, wr):
        for k in wr:
            last[k] = tok
            readers[k] = {}
        for k in rd:
            readers.setdefault(k, {})[tok[0]] = tok

    def split(keys):
        return keys.split() if keys else []

    def op(q, name, args, rd="", wr="", **kw):
        rd, wr, own = split(rd), split(wr), "q" + q
        before(q, own, rd, wr)
        eng = queue[q]
        fns = {"copy": ("v", lambda: eng.tensor_copy(*args)), "tt": ("v", lambda: eng.tensor_tensor(*args)),
               "ts": ("v", lambda: eng.tensor_scalar(*args)), "act": ("s", lambda: eng.activation(*args, **kw)),
               "mm": ("p", lambda: eng.matmul(*args)), "scan": ("v", lambda: eng.tensor_tensor_scan(*args)),
               "red": ("v", lambda: eng.tensor_reduce(*args)), "set": ("v", lambda: eng.memset(*args)),
               "iota": ("g", lambda: eng.iota(*args, **kw))}
        fns[name][1]().then_inc(T.sem[own], 1)
        count[own] = count.get(own, 0) + 1
        after((own, count[own], dict(seen[q])), rd, wr)

    dmas = [0]

    def dma(q, out, in_, rd="", wr=""):
        rd, wr = split(rd), split(wr)
        s = "d%d" % dmas[0]
        dmas[0] += 1
        before(q, s, rd, wr)
        queue[q].dma_start(out, in_).then_inc(T.sem[s], 16)
        count[s] = 16
        after((s, 16, dict(seen[q])), rd, wr)

    def mm(out, lhs, rhs, start, stop, rd, wr):
        op("p", "mm", (out, lhs, rhs, start, stop), rd, wr)

    dma("y", T.AR[:, 0:256], T.rf[0::16, :], wr="AR0")
    dma("y", T.AR[:, 256:512], T.an[:, :], wr="AR1")
    dma("y", T.WI[:], T.w[:], wr="WI")
    dma("y", T.TI[:], T.th[:], wr="TI")
    dma("y", T.XW[:, 0:4096], T.xc[:], wr="X1")
    dma("y", T.XW[:, 8192:12288], T.xc[:], wr="X3")
    for h in range(2):
        dma("y", T.RI[:, 2048 * h:2048 * h + 2048], T.rf[:, 2048 * h:2048 * h + 2048], wr="RI%d" % h)

    op("g", "iota", (T.PI[:], [[0, 1]], 0, 1), wr="PI")
    op("g", "iota", (T.CI[:], [[1, 144]], 0, 0), wr="CI")
    op("g", "iota", (T.VI[:], [[256, 16]], 0, 16), wr="VI")
    op("g", "iota", (T.KI[:], [[16, 16]], 256, 1), wr="KI")
    op("g", "iota", (T.LOW[:], [[0, 64], [1, 64]], 0, 0), wr="LOW", allow_small_or_imprecise_dtypes=True)
    op("g", "iota", (T.IOT[:], [[1, 64], [0, 64]], 0, 0), wr="IOT", allow_small_or_imprecise_dtypes=True)

    ncol = {}

    def col(name):
        if name not in ncol:
            ncol[name] = len(ncol)
        return T.COL[:, ncol[name]:ncol[name] + 1]

    def ts(out, in0, s1, s2, o0, o1, rd, wr):
        op("v", "ts", (out, in0, s1, s2, o0) if o1 is None else (out, in0, s1, s2, o0, o1), rd, wr)

    def tt(out, a, b, o, rd, wr):
        op("v", "tt", (out, a, b, o), rd, wr)

    def cp(out, in_, rd, wr):
        op("v", "copy", (out, in_), rd, wr)

    SVall = "SV0 SV1 SV2 SV3 SVx"
    Xall = "X1 X2 X3"
    op("v", "set", (T.SV[:], 1.0), wr=SVall)
    op("s", "act", (T.AW[:, 0:4096], T.SV[:], F.Copy), SVall, "AW AWr")
    op("v", "set", (T.ARB[:, 1024:1040], 0.0), wr="pad")
    ts(T.ARS[:, 0:512], T.AR[:], 6, None, A.arith_shift_right, None, "AR0 AR1", "ARS0")
    ts(T.ARS[:, 512:1024], T.AR[:], 63, None, A.bitwise_and, None, "AR0 AR1", "ARS1")
    cp(T.ARB[:, 0:1024], T.ARS[:], "ARS0 ARS1", "ARB")
    dma("y", T.SV[0::16, :], T.ARB[:, 0:256], rd="ARB", wr="SV0")
    dma("y", T.SV[1::16, :], T.ARB[:, 512:768], rd="ARB", wr="SV1")
    dma("y", T.SV[2::16, :], T.ARB[:, 257:513], rd="ARB", wr="SV2")
    dma("y", T.SV[3::16, :], T.ARB[:, 769:1025], rd="ARB pad", wr="SV3")
    dma("y", T.AW[0::16, 0:4096], T.ARB[:, 256:512], rd="ARB", wr="AW")
    dma("y", T.AW[1::16, 0:4096], T.ARB[:, 768:1024], rd="ARB", wr="AWr")
    dma("y", T.IOT[1::16, :], T.LOW[0:8, :], rd="LOW", wr="IOT")
    op("v", "copy", (col("p"), T.PI[:]), "PI", "c_p")
    ts(T.PGI[:], T.PI[:], 112, None, A.bitwise_and, None, "PI", "PGI")
    ts(T.PKI[:], T.PI[:], 15, None, A.bitwise_and, None, "PI", "PKI")
    ts(T.MG[:], T.CI[:, 0:128], 112, None, A.bitwise_and, None, "CI", "MG")
    cp(col("pg"), T.PGI[:], "PGI", "c_pg")
    ts(col("pg16"), T.PGI[:], 16.0, None, A.add, None, "PGI", "c_pg16")
    ts(col("pgx"), T.PGI[:], 16.0, None, A.mult, None, "PGI", "c_pgx")
    ts(col("k0"), T.PKI[:], 0.0, 64.0, A.is_equal, A.mult, "PKI", "c_k0")
    ts(col("k1"), T.PKI[:], 1.0, None, A.is_equal, None, "PKI", "c_k1")
    ts(col("k2"), T.PKI[:], 2.0, 64.0, A.is_equal, A.mult, "PKI", "c_k2")
    ts(col("k3"), T.PKI[:], 3.0, None, A.is_equal, None, "PKI", "c_k3")
    ts(col("k4"), T.PKI[:], 4.0, NEG, A.is_equal, A.mult, "PKI", "c_k4")
    ts(col("k5"), T.PKI[:], 5.0, 4096.0, A.is_equal, A.mult, "PKI", "c_k5")
    ts(col("nk"), T.PKI[:], 0.0, None, A.is_gt, None, "PKI", "c_nk")
    ts(T.KCI[:], T.PKI[:], 613.0, None, A.mult, None, "PKI", "KCI")
    tt(col("kr"), col("k0"), col("k1"), A.add, "c_k0 c_k1", "c_kr")
    tt(col("kb"), col("k2"), col("k3"), A.add, "c_k2 c_k3", "c_kb")
    ts(T.BI[:], T.KCI[:], 4095, None, A.bitwise_and, None, "KCI", "BI")
    tt(col("k45"), col("k4"), col("k5"), A.add, "c_k4 c_k5", "c_k45")
    cp(col("kc"), T.BI[:], "BI", "c_kc")
    tt(col("kk"), col("kr"), col("k45"), A.add, "c_kr c_k45", "c_kk")
    ts(T.IDM[:], T.CI[:, 0:128], col("p"), None, A.is_equal, None, "CI c_p", "IDM")
    ts(T.NID[:], T.CI[:, 0:128], col("p"), -1.0, A.is_equal, A.mult, "CI c_p", "NID")
    ts(T.BLK[:], T.MG[:], col("pg"), None, A.is_equal, None, "MG c_pg", "BLK")
    ts(T.SVR[:], T.MG[:], col("pg"), col("kr"), A.is_equal, A.mult, "MG c_pg c_kr", "SVR")
    cp(col("w"), T.WI[:], "WI", "c_w")
    ts(col("th"), T.TI[:], 8192.0, NEG, A.mult, A.add, "TI", "c_th")
    ts(T.WM[:], T.MG[:], col("pg"), col("w"), A.is_equal, A.mult, "MG c_pg c_w", "WM")
    ts(T.SVK[:], T.MG[:], col("pg"), col("kk"), A.is_equal, A.mult, "MG c_pg c_kk", "SVK")
    ts(T.Z8[:], T.CI[:], col("pg16"), 8192.0, A.is_equal, A.mult, "CI c_pg16", "Z8")

    def prep_u(c):
        mm(T.M1[:, 0:256], T.WM[:], T.XW[:, c:4096:16], True, True, "WM X1", "#M1")
        mm(T.M1[:, 256:512], T.SVR[:], T.SV[:, c::16], True, True, "SVR " + SVall, "#M1")

    def prep_v(c):
        cp(T.UC[:], T.M1[:, 0:256], "#M1", "UC")
        ts(T.UT[:, c::16], T.UC[:], 4095, None, A.bitwise_and, None, "UC", "UT")
        tt(T.OA[:], T.M1[:, 256:512], T.UT[:, c::16], A.mult, "#M1 UT", "OA")
        ts(T.OB[:], T.OA[:], 5, 4095, A.arith_shift_right, A.bitwise_and, "OA", "OB")
        tt(T.OC[:], T.M1[:, 256:512], T.OB[:], A.add, "#M1 OB", "OC")
        ts(T["PLO%d" % (c % 2)][:], T.OC[:], col("kc"), None, A.add, None, "OC c_kc", "PLO%d" % (c % 2))

    turn = [0]

    def gather(e, c, q, b=0):
        G, pl = (T.GE, "PLE") if e else (T.GO, "PLO%d" % (b % 2))
        src = T.XW[:].indirect(T[pl][:, 64 * c:64 * c + 64])
        out = G[:, 1024 * c:1024 * c + 1024]
        key = ("GE%d" if e else "GO%d") % c
        if q == "v":
            cp(out, src, Xall + " " + pl, key)
        else:
            op("s", "act", (out, src, F.Copy), Xall + " " + pl, key)

    pending = []

    def sums(item):
        e, c, w, b = item
        K, key = (T.KE, "#KE") if e else (T.KO, "#KO")
        o = K[:, 64 * c:64 * c + 64]
        for h in range(2):
            if h == 0 and e:
                mm(o, T.SVE[:], T.SVG[:, 64 * c:64 * c + 64], True, False, "SVE SVG", key)
                mm(o, T.DNM[:], T.EG[:, 64 * c:64 * c + 64], False, False, "DNM EG", key)
            elif h == 0:
                mm(o, T.SVK[:], T.SV[:, 1024 * c + b:1024 * c + 1024:16], True, False, "SVK " + SVall, key)
            for k in range(8 * h, 8 * h + 8):
                mm(o, T.Z8[:, 16 - k:144 - k], T["AB%d" % w][:, 64 * k:64 * k + 64], False, k == 15, "Z8 AB%d_%d" % (w, h), key)

    def diff(e, c, b=0, halves=False):
        w = turn[0] % 2
        turn[0] += 1
        G, key = (T.GE, "GE%d" % c) if e else (T.GO, "GO%d" % c)
        q, qk = (T.QG[:, 64 * c:64 * c + 64], "QG") if e else (T.XW[:, 1024 * c + b:1024 * c + 1024:16], "X1")
        W, AB = T["W%d" % w], T["AB%d" % w]
        for k in range(16):
            o, wk = W[:, 64 * k:64 * k + 64], "#W%d_%d" % (w, k // 8)
            mm(o, T.IDM[:], G[:, 1024 * c + k:1024 * c + 1024:16], True, False, "IDM " + key, wk)
            mm(o, T.NID[:], q, False, True, "NID " + qk, wk)
            if halves and k % 8 == 7:
                h = k // 8
                op("s", "act", (AB[:, 512 * h:512 * h + 512], W[:, 512 * h:512 * h + 512], F.Abs), wk, "AB%d_%d" % (w, h))
        if not halves:
            op("s", "act", (AB[:], W[:], F.Abs), "#W%d_0 #W%d_1" % (w, w), "AB%d_0 AB%d_1" % (w, w))
        pending.append((e, c, w, b))
        while len(pending) > 1:
            sums(pending.pop(0))

    def flush():
        while pending:
            sums(pending.pop(0))

    def own_unit(b, hooks):
        for c in range(CH + 1):
            for at, f in hooks:
                if at == c:
                    f()
            if c < CH:
                gather(False, c, "v" if c in O_ON_V else "s", b)
            if c:
                diff(False, c - 1, b)

    def own_table(b):
        op("s", "act", (T.KOT[:, b::16], T.KO[:, 0:256], F.Copy), "#KO", "KOT")

    def wrap(o, Z, src, zk, sk):
        for il in range(16):
            mm(o, Z[:, 16 - il:144 - il], src(il), il == 0, il == 15, zk + " " + sk, "#M2")

    CNT, AAW, AVW, TRI_, TOT, FITS = (T.M2[:, 256 + 16 * j:272 + 16 * j] for j in range(6))

    def smalls():
        op("s", "act", (T.QG[:], T.XW[:, 0:4096].indirect(T.V16[:]), F.Copy), "X1 V16", "QG")
        op("s", "act", (T.AWG[:], T.AW[:, 0:4096].indirect(T.A16[:]), F.Copy), "AW AWr A16", "AWG")
        op("s", "act", (T.SVG[:], T.SV[:].indirect(T.V16[:]), F.Copy), SVall + " V16", "SVG")

    def wraps():
        wrap(AVW, T.ZB, lambda il: T.SVG[:, il::16], "ZB", "SVG")
        wrap(AAW, T.ZA, lambda il: T.AWG[:, il::16], "ZA", "AWG")
        op("s", "act", (T.AAS[:], AAW, F.Copy), "#M2", "AAS")

    def fits():
        op("s", "act", (T.JK[:], FITS, F.Copy), "#M2", "JK c_bs", accum_out=col("bs"))

    def place_e():
        tt(T.TA[:], T.RW[:, 0:4096].indirect(T.A16[:]), T.UG[:], A.mult, "RW A16 UG", "TA")
        op("s", "act", (T.EG[:], T.RW[:, 0:4096].indirect(T.A16[:]), F.Copy), "RW A16", "EG")
        ts(T.TB[:], T.TA[:], 5, 4095, A.arith_shift_right, A.bitwise_and, "TA", "TB")
        tt(T.TC[:], T.RW[:, 0:4096].indirect(T.A16[:]), T.TB[:], A.add, "RW A16 TB", "TC")
        ts(T.PLE[:], T.TC[:], col("kc"), None, A.add, None, "TC c_kc", "PLE")

    def merge(t):
        cp(T.RW[:, 8 + t:4096:64], T.LAND[:, 64 * t:64 * t + 64], "LAND%d" % t, "RW")

    def keep_yh(t):
        op("s", "act", (T.YH[:, t::8], T.LAND[:, 64 * t:64 * t + 64], F.Copy), "LAND%d" % t, "YH")

    def gathers_e():
        for c in E_ON_S:
            gather(True, c, "s")
        for c in range(CH):
            if c not in E_ON_S:
                gather(True, c, "v")

    prep_u(0)
    prep_v(0)
    ts(T.ZA[:], T.CI[:], col("pg16"), col("kr"), A.is_equal, A.mult, "CI c_pg16 c_kr", "ZA")
    ts(T.VF0[:], T.VI[:], col("pgx"), None, A.subtract, None, "VI c_pgx", "VF0")
    wrap(AAW, T.ZA, lambda il: T.AW[:, 16 * il:4096:256], "ZA", "AW AWr")
    op("s", "act", (T.XW[:, 4096:8192], T.XW[:, 0:4096], F.Copy), "X1", "X2")
    cp(T.V16[:], T.VF0[:], "VF0", "V16")
    cp(T.UG[:], T.UT[:, 0:4096].indirect(T.V16[:]), "UT V16", "UG")
    cp(T.A16[:], AAW, "#M2", "A16")
    for h in range(2):
        cp(T.RW[:, 2048 * h:2048 * h + 2048], T.RI[:, 2048 * h:2048 * h + 2048], "RI%d" % h, "RW")
    own_unit(0, [(3, smalls), (4, place_e), (4, gathers_e)])
    ts(T.T0[:], T.MG[:], col("pg"), col("k4"), A.is_equal, A.mult, "MG c_pg c_k4", "T0")
    ts(T.T1[:], T.CI[:, 0:128], col("pg"), col("kr"), A.is_equal, A.mult, "CI c_pg c_kr", "T1")
    tt(T.SVE[:], T.T0[:], T.T1[:], A.add, "T0 T1", "SVE")
    ts(T.DNM[:], T.CI[:, 0:128], col("p"), col("nk"), A.is_equal, A.mult, "CI c_p c_nk", "DNM")
    ts(T.T0[:], T.MG[:], col("p"), None, A.is_equal, None, "MG c_p", "T0")
    tt(T.EQM[:], T.IDM[:], T.T0[:], A.subtract, "IDM T0", "EQM")
    ts(T.ZB[:], T.CI[:], col("pg16"), col("kb"), A.is_equal, A.mult, "CI c_pg16 c_kb", "ZB")
    prep_u(1)
    prep_v(1)
    op("v", "set", (T.ALL1[:], 1.0), wr="ALL1")
    op("v", "set", (T.ZERO[:], 0.0), wr="ZERO")
    op("v", "set", (T.SC[:], 0.0), wr="SC")
    ts(T.Z1[:], T.CI[:], col("pg16"), None, A.is_equal, None, "CI c_pg16", "Z1")
    ts(T.T1[:], T.CI[:, 0:128], col("p"), None, A.is_gt, None, "CI c_p", "T1")
    tt(T.TRI[:], T.T1[:], T.BLK[:], A.mult, "T1 BLK", "TRI")
    ts(T.KD[:], T.KI[:], col("pg"), 1.0 / 4096, A.subtract, A.mult, "KI c_pg", "KD")
    for t in range(NST):
        op("s", "act", (T.PRES[:, 64 * t:64 * t + 64], T.RW[:, 8 + t:4096:64], F.Copy), "RW", "PRES%d" % t)
    before("g", "pre", ["PRES%d" % t for t in range(NST)], [])
    trs = []
    for t in range(NST):
        src = T.cores[(rank - 1 - t % (n_ranks - 1)) % n_ranks]
        rid, pid = topo.addr(src)[:2]
        e = topo.engines(core, src)
        trs.append(RemoteDMATransfer(dst_ids=[DstId(rid=rid, pnc=pid)], dma_engine_mask=1 << e[t % len(e)], remote_sem=T.sem.pre,
                                     src=T.PRES[:, 64 * t:64 * t + 64], dst=T.CB[:, CBW * t:CBW * t + 64]))
    g.remote_dma_fused(trs, local_sem=T.sem.sent)
    sent = NST
    after(("pre", NST, {}), [], ["CB%d" % t for t in range(NST)])
    count["pre"] = NST

    for t in range(NST):
        lastep = t == NST - 1
        vf, vn = T["VF%d" % (t % 2)], T["VF%d" % ((t + 1) % 2)]
        vfk, vnk = "VF%d" % (t % 2), "VF%d" % ((t + 1) % 2)
        if t > 0 and t + 1 < NST:
            prep_u(t + 1)
            prep_v(t + 1)
        if t > 0:
            cp(T.BI[:], col("bs"), "c_bs", "BI")
            ts(T.BI2[:], T.BI[:], 255, None, A.bitwise_and, None, "BI", "BI2")
            ts(col("thb"), T.BI2[:], 8192.0, col("th"), A.mult, A.add, "BI2 c_th", "c_thb")
        order = [c for c in E_ON_S] + [c for c in range(CH) if c not in E_ON_S]
        for c in order:
            diff(True, c, 0, c == order[-1])
            if c == order[0]:
                own_table(t)
                op("s", "act", (T.IOG[:], T.IOT[:].indirect(T.A16[:]), F.Copy), "IOT A16", "IOG")
            if c == order[EQ_AFTER]:
                if t == 0:
                    wraps()
                mm(T.M2[:, 0:256], T.EQM[:], T.EG[:], True, True, "EQM EG", "#M2")
                op("s", "act", (T.NEQ[:], T.M2[:, 0:256], F.Abs), "#M2", "NEQ", scale=33554432.0)
        flush()
        tt(T.DM[:], T.KOT[:].indirect(T.V16[:]), T.NEQ[:], A.add, "KOT V16 NEQ", "DM")
        tt(T.DA[:], AVW, T.AAS[:], A.subtract, "#M2 AAS", "DA")
        tt(T.MN[:], T.KE[:, 0:256], T.DM[:], A.min, "#KE DM", "MN")
        ts(T.IND[:], T.MN[:], col("th" if t == 0 else "thb"), None, A.is_lt, None, "MN " + ("c_th" if t == 0 else "c_thb"), "IND")
        ts(T.FV[:], T.MN[:], 4095, None, A.bitwise_and, None, "MN", "FV")
        wrap(CNT, T.Z1, lambda il: T.IND[:, il::16], "Z1", "IND")
        ts(T.FW[:], CNT, 7.5, None, A.is_gt, None, "#M2", "FW")
        ts(T.NF[:], CNT, 7.5, 4096.0, A.is_lt, A.mult, "#M2", "NF")
        mm(TOT, T.BLK[:], T.FW[:], True, True, "BLK FW", "#M2")
        mm(TRI_, T.TRI[:], T.FW[:], True, True, "TRI FW", "#M2")
        if not lastep:
            mm(FITS, T.ALL1[:], T.FW[:], True, True, "ALL1 FW", "#M2")
        tt(T.GD[:], T.NF[:], T.KD[:], A.mult, "NF KD", "GD")
        op("v", "scan", (T.SC[:, 1:17], TOT, T.ZERO[:], 0.0, A.add, A.add), "#M2 ZERO SC", "SC")
        tt(T.P1[:], TRI_, T.GD[:], A.add, "#M2 GD", "P1")
        tt(T.DD[:], vf[:], T.NF[:], A.add, vfk + " NF", "DD")
        tt(T.P2[:], T.P1[:], T.SC[:, 0:16], A.add, "P1 SC", "P2")
        tt(T.MA[:], T.FW[:], T.DA[:], A.mult, "FW DA", "MA")
        cp(T.C16[:], T.P2[:], "P2", "C16")
        cp(T.D16[:], T.DD[:], "DD", "D16")
        cp(T.CB[:, CBW * t:CBW * t + CBW].indirect(T.C16[:]), T.FV[:], "C16 FV CB%d" % t, "CB%d" % t)
        dst = T.cores[(rank + 1 + t % (n_ranks - 1)) % n_ranks]
        rid, pid = topo.addr(dst)[:2]
        ne = len(topo.engines(core, dst))
        before("g", "x", ["CB%d" % t], [])
        g.remote_dma(T.LAND[:, 64 * t:64 * t + 64], T.CB[:, CBW * t:CBW * t + 64], T.sem["arr%d" % t], T.sem.sent, pid, rid, topo.mask(core, dst))
        sent += ne
        after(("arr%d" % t, ne, {}), [], ["LAND%d" % t])
        count["arr%d" % t] = ne
        if lastep:
            cp(T.RW[:].indirect(T.D16[:]), T.FV[:], "D16 FV", "RW")
        tt(T.AN[:], T.MA[:], T.AAS[:], A.add, "MA AAS", "AN")
        tt(vn[:], vf[:], T.FW[:], A.add, vfk + " FW", vnk)
        cp(T.AW[:].indirect(T.D16[:]), T.IOG[:], "D16 IOG", "AW AWr")
        cp(T.A16[:], T.AN[:], "AN", "A16")
        cp(T.V16[:], vn[:], vnk, "V16")
        if not lastep:
            cp(T.RW[:].indirect(T.D16[:]), T.FV[:], "D16 FV", "RW")
            cp(T.UG[:], T.UT[:, 0:4096].indirect(T.V16[:]), "UT V16", "UG")
            own_unit(t + 1, [(2, fits), (HOOK, smalls), (WHOOK, wraps), (EHOOK, lambda: merge(t)), (EHOOK, place_e), (EHOOK, gathers_e), (4, lambda: keep_yh(t))])

    for s in range(4):
        w, h = s // 2, s % 2
        o, wk = T["W%d" % w][:, 512 * h:512 * h + 256], "#W%d_%d" % (w, h)
        op("s", "act", (o, T.RW[:, 4 + s:4096:16], F.Copy), "RW", wk, scale=4096.0)
        tt(T.KOT[:, s:1024:4], o, T.RW[:, s:4096:16], A.add, "RW " + wk, "YR%d" % s)
    dma("y", T.yr[:], T.KOT[:, 0:1024], rd="YR0 YR1 YR2 YR3")
    op("s", "act", (T.IOG[:], T.IOT[:].indirect(T.A16[:]), F.Copy), "IOT A16", "IOG")
    cp(T.SVG[:], T.IOT[:].indirect(T.V16[:]), "IOT V16", "SVG")
    keep_yh(NST - 1)
    dma("y", T.yh[:], T.YH[:], rd="YH")
    for s in range(8):
        w, h = s // 2 % 2, s % 2
        o, wk = T["W%d" % w][:, 512 * h:512 * h + 256], "#W%d_%d" % (w, h)
        mm(o, T.SVR[:], T.AW[:, s:4096:16], True, True, "SVR AW AWr", wk)
        if h:
            op("s", "act", (T.KOT[:, 2048 + s::8], o, F.Copy), wk, "YAN%d" % s)
        else:
            cp(T.KOT[:, 2048 + s::8], o, wk, "YAN%d" % s)
    mm(T.KO[:, 0:256], T.SVR[:], T.SVG[:], True, True, "SVR SVG", "#KO")
    mm(T.KO[:, 256:512], T.SVR[:], T.IOG[:], True, True, "SVR IOG", "#KO")
    op("s", "act", (T.YVA[:], T.KO[:], F.Copy), "#KO", "YVA")
    dma("y", T.yan[:], T.KOT[0::16, 2048:4096], rd=" ".join("YAN%d" % s for s in range(8)))
    dma("y", T.yv[:], T.YVA[0::16, 0:256], rd="YVA")
    dma("y", T.ya[:], T.YVA[0::16, 256:512], rd="YVA")
    count["sent"] = sent
    for s in count:
        if seen["g"].get(s, 0) < count[s]:
            g.wait_ge(T.sem[s], count[s])
